import numpy as np
import ml_dtypes


def mxq(x, axis, fmt="e4m3"):
    dtype, down = {"e4m3": (ml_dtypes.float8_e4m3fn, 7), "e5m2": (ml_dtypes.float8_e5m2, 14)}[fmt]
    v = np.moveaxis(np.asarray(x, np.float32).astype(ml_dtypes.bfloat16).astype(np.float64), axis, -1)
    blocks = v.reshape(v.shape[:-1] + (-1, 32))
    amax = np.abs(blocks).max(-1, keepdims=True)
    byte = np.maximum(np.where(amax > 0, np.frexp(amax)[1] - 1 + 127, 0) - down, 1)
    scale = np.exp2(byte - 127.0)
    codes = (blocks / scale).astype(np.float32).astype(dtype).astype(np.float64)
    return np.moveaxis((codes * scale).reshape(v.shape), -1, axis)


WIDE = False


def mx_kscale(k):
    if not WIDE:
        return np.ones(k)
    levels = np.array([24, -24, 12, -12, 0])
    if k % 512:
        return np.exp2(np.random.permutation(np.resize(levels, k // 32))).repeat(32)
    a = np.empty((k // 512, 16))
    for p in range(k // 512):
        a[p, :8] = np.random.permutation(np.resize(levels, 8))
        for g in range(8):
            far = levels[np.abs(levels - a[p, g]) >= 10]
            a[p, g + 8] = far[np.random.randint(len(far))]
    return np.exp2(a.ravel()).repeat(32)


def f64(x):
    return np.asarray(x).astype(np.float64)


def striped8(idx):
    return np.concatenate([v.reshape(-1, 16).T for v in idx]).astype(np.uint16)


def unstriped8(offs):
    return np.stack([offs[16 * g:16 * g + 16].T.reshape(-1) for g in range(8)]).astype(np.int64)


E2M1 = np.array([0.0, 0.5, 1.0, 1.5, 2.0, 3.0, 4.0, 6.0, -0.0, -0.5, -1.0, -1.5, -2.0, -3.0, -4.0, -6.0])


def pack_weight(w, fmt):
    k, n = w.shape
    w = f64(np.asarray(w, np.float32).astype(ml_dtypes.bfloat16)).reshape(k // 32, 32, n)
    amax = np.abs(w).max(1)
    if fmt == "e4m3":
        byte = np.frexp(amax)[1] - 1 + 127 - 7
    else:
        mant, ex = np.frexp(amax / 6.0)
        byte = np.where(mant > 0.5, ex, ex - 1) + 127
    byte = np.clip(np.where(amax > 0, byte, 1), 1, 254)
    scaled = (w * np.exp2(127.0 - byte)[:, None, :]).reshape(k, n).astype(np.float32)
    by_word = np.ascontiguousarray(scaled.reshape(k // 512, 128, 4, n).transpose(0, 1, 3, 2))
    if fmt == "e4m3":
        words = by_word.astype(ml_dtypes.float8_e4m3fn).view(np.uint8)
    else:
        c = by_word.astype(ml_dtypes.float4_e2m1fn).view(np.uint8) & 0xF
        words = (c[..., 0::2] | (c[..., 1::2] << 4)).reshape(k // 512, 128, 2 * n)
    return np.ascontiguousarray(words), np.ascontiguousarray(byte.astype(np.uint8).reshape(k // 512, 16, n))


def unpack_weight(words, scales, fmt):
    g, _, n = scales.shape
    words = np.ascontiguousarray(words).reshape(g, 128, n, -1)
    if fmt == "e4m3":
        vals = words.view(ml_dtypes.float8_e4m3fn).astype(np.float64)
    else:
        nib = np.empty((g, 128, n, 4), np.uint8)
        nib[..., 0::2] = words & 0xF
        nib[..., 1::2] = words >> 4
        vals = E2M1[nib]
    vals = vals * np.repeat(np.exp2(scales.astype(np.float64) - 127.0), 8, axis=1)[..., None]
    return vals.transpose(0, 1, 3, 2).reshape(g * 512, n)


def gelu(f):
    return 0.5 * f * (1.0 + np.tanh(np.sqrt(2.0 / np.pi) * (f + 0.044715 * f**3)))


K, L, N, T, J = 512, 512, 512, 2048, 1024


def setup_inputs():
    n = np.random.standard_normal
    s = mx_kscale(K)[:, None]
    s2 = mx_kscale(L)[:, None]
    p_wt = pack_weight(n((K, N)) / np.sqrt(K) / s, "e2m1")
    p_wx = pack_weight(n((L, N)) / np.sqrt(L) / s2, "e4m3")
    return {
        "xT": (n((K, T)) * s).astype(np.float32),
        "wgt": np.repeat(np.random.uniform(0.5, 2.0, (8, J)), 16, axis=0).astype(np.float32),
        "wt_words": p_wt[0],
        "wt_scales": p_wt[1],
        "c": (n((L, J)) * s2).astype(np.float32),
        "wx_words": p_wx[0],
        "wx_scales": p_wx[1],
        "b": (0.3 * n(N)).astype(np.float32),
        "offs": striped8(np.stack([np.random.permutation(T)[:J] for _ in range(8)])),
    }


def reference(xT, wgt, wt_words, wt_scales, c, wx_words, wx_scales, b, offs):
    idx = unstriped8(offs)
    rows = np.arange(K)
    xg = f64(wgt)[rows // 4 % 128] * f64(xT)[rows[:, None], idx[rows % 512 // 64]]
    xT_ = mxq(xg, 0, "e4m3")
    wt_ = unpack_weight(wt_words, wt_scales, "e2m1")
    c_q_ = mxq(f64(c), 0, "e4m3")
    c_r_ = mxq(f64(c) - c_q_, 0, "e4m3")
    wx_ = unpack_weight(wx_words, wx_scales, "e4m3")
    y = wt_.T @ xT_ + wx_.T @ c_q_ + wx_.T @ c_r_
    return gelu(y + f64(b)[:, None])

@@ -1,0 +1,257 @@
+from contextlib import ExitStack
+
+import concourse.mybir as mybir
+from concourse.masks import make_identity
+
+K, L, N, T, J = 512, 512, 512, 2048, 1024
+FLOPS = 2 * N * J * (K + 2 * L) + 2 * L * L * J
+
+F32 = mybir.dt.float32
+BF16 = mybir.dt.bfloat16
+I32 = mybir.dt.int32
+U32 = mybir.dt.uint32
+U16 = mybir.dt.uint16
+U8 = mybir.dt.uint8
+FP8X4 = mybir.dt.float8_e4m3fn_x4
+FP4X4 = mybir.dt.float4_e2m1fn_x4
+ALU = mybir.AluOpType
+GELU = mybir.ActivationFunctionType.Gelu_apprx_tanh
+
+P = 128
+PACK = 4
+CHUNK = 256
+CHUNKS = J // CHUNK
+HALF = J // 2
+STRIP = 128
+RUN = 4
+EARLY = 2
+WEAVE_ON_VECTOR = (2,)
+
+
+def tile_list_gelu_kernel(
+    tc, xT, wgt, wt_words, wt_scales, c, wx_words, wx_scales, b, offs, out
+):
+    nc = tc.nc
+    with ExitStack() as ctx:
+        keep = ctx.enter_context(tc.tile_pool(name="keep", bufs=1))
+        psum = ctx.enter_context(tc.psum_pool(name="psum", bufs=1))
+
+        def mx_tiles(name, width):
+            codes = keep.tile([P, width], U32, name=name + "_codes", align_bytes=64)
+            scales = keep.tile([P, width], U8, name=name + "_scales", align_bytes=64)
+            return codes, scales
+
+        def quantize(operand, woven):
+            codes, scales = operand
+            nc.vector.quantize_mx(
+                out=codes[:].bitcast(FP8X4), scales=scales[:], in_=woven[:].rearrange("p j t -> p (j t)")
+            )
+
+        def by_runs_planes(planes):
+            return planes.rearrange("p t (c i) -> p c t i", i=RUN)
+
+        def by_runs_woven(woven):
+            return woven.rearrange("p (c i) t -> p c t i", i=RUN)
+
+        offsets = keep.tile([P, J // 16], U16, name="offsets")
+        x_planes = [keep.tile([P, T], F32, name="x%d" % t) for t in range(PACK)]
+        wgt_sb = [keep.tile([P, HALF], F32, name="wgt%d" % h) for h in range(2)]
+        c_sb = [keep.tile([P, PACK, CHUNK], F32, name="c%d" % q) for q in range(CHUNKS)]
+        wt_sb = keep.tile([P, 2 * N], U8, name="wt_sb", align_bytes=64)
+        wx_sb = keep.tile([P, N], U32, name="wx_sb", align_bytes=64)
+        wt_sc = keep.tile([P, N], U8, name="wt_sc", align_bytes=64)
+        wx_sc = keep.tile([P, N], U8, name="wx_sc", align_bytes=64)
+        bias = keep.tile([P, N // P], F32, name="bias")
+        eye = keep.tile([P, L, PACK], BF16, name="eye", align_bytes=64)
+        eye_q = mx_tiles("eye", L)
+
+        nc.vector.memset(eye[:].rearrange("p m t -> p (m t)"), 0.0)
+        nc.vector.memset(wx_sc[:].bitcast(I32), 0)
+        nc.vector.memset(wt_sc[:].bitcast(I32), 0)
+        ident = keep.tile([P, P], BF16, name="ident")
+        make_identity(nc, ident[:])
+        for t in range(PACK):
+            nc.vector.tensor_copy(out=eye[:, t * P : (t + 1) * P, t], in_=ident[:])
+
+        c_rows = c.rearrange("(p t) j -> p t j", t=PACK)
+        x_rows = xT.rearrange("(p t) s -> p t s", t=PACK)
+
+        def load_c(q):
+            nc.sync.dma_start(out=c_sb[q][:], in_=c_rows[:, :, q * CHUNK : (q + 1) * CHUNK])
+
+        def load_x(t):
+            nc.sync.dma_start(out=x_planes[t][:], in_=x_rows[:, t, :])
+
+        def load_wgt(h):
+            nc.sync.dma_start(out=wgt_sb[h][:], in_=wgt[:, h * HALF : (h + 1) * HALF])
+
+        def load_scales(plane, rows, quadrants):
+            for quad in quadrants:
+                nc.sync.dma_start(
+                    out=plane[32 * quad : 32 * quad + 4, :].bitcast(I32),
+                    in_=rows[0, 4 * quad : 4 * quad + 4, :].bitcast(I32),
+                )
+
+        for q in range(EARLY):
+            load_c(q)
+        load_wgt(0)
+        nc.sync.dma_start(offsets[:], offs)
+        load_x(0)
+        load_wgt(1)
+        load_scales(wx_sc, wx_scales, (0, 1))
+        load_x(1)
+        nc.sync.dma_start(out=wx_sb[:].bitcast(I32), in_=wx_words[0].rearrange("p n t -> p (n t)").bitcast(I32))
+        load_scales(wx_sc, wx_scales, (2, 3))
+        load_x(2)
+        load_scales(wt_sc, wt_scales, (0, 1))
+        load_x(3)
+        load_scales(wt_sc, wt_scales, (2, 3))
+        nc.sync.dma_start(out=wt_sb[:].bitcast(I32), in_=wt_words[0].bitcast(I32))
+        with nc.allow_non_contiguous_dma(reason="one bias value for each partition"):
+            nc.sync.dma_start(out=bias[:], in_=b.rearrange("(u p) -> p u", p=P))
+        for q in range(EARLY, CHUNKS):
+            load_c(q)
+
+        quantize(eye_q, eye)
+
+        c_q = [mx_tiles("cq%d" % q, CHUNK) for q in range(CHUNKS)]
+        c_r = [mx_tiles("cr%d" % q, CHUNK) for q in range(CHUNKS)]
+        x_q = [mx_tiles("xq%d" % q, CHUNK) for q in range(CHUNKS)]
+        picked = [keep.tile([P, PACK, HALF], F32, name="picked%d" % h) for h in range(2)]
+        left = {}
+
+        def first_tier(q):
+            woven = keep.tile([P, CHUNK, PACK], BF16, name="c_woven%d" % q, align_bytes=64)
+            nc.scalar.copy(out=by_runs_woven(woven[:]), in_=by_runs_planes(c_sb[q][:]))
+            quantize(c_q[q], woven)
+
+        def left_over(q):
+            left[q] = keep.tile([P, CHUNK, PACK], BF16, name="left%d" % q, align_bytes=64)
+            for s in range(CHUNK // STRIP):
+                cols = slice(s * STRIP, (s + 1) * STRIP)
+                back = psum.tile([P, PACK, STRIP], F32, name="back", tag="back", bufs=2)
+                for t in range(PACK):
+                    rows = slice(t * P, (t + 1) * P)
+                    nc.tensor.matmul_mx(
+                        out=back[:, t, :],
+                        lhsT=eye_q[0][:, rows].bitcast(FP8X4),
+                        lhsT_scale=eye_q[1][:, rows],
+                        rhs=c_q[q][0][:, cols].bitcast(FP8X4),
+                        rhs_scale=c_q[q][1][:, cols],
+                        start=True,
+                        stop=True,
+                    )
+                nc.vector.tensor_tensor(
+                    out=by_runs_woven(left[q][:, cols, :]),
+                    in0=by_runs_planes(c_sb[q][:, :, cols]),
+                    in1=by_runs_planes(back[:]),
+                    op=ALU.subtract,
+                )
+
+        def second_tier(q):
+            quantize(c_r[q], left[q])
+
+        def pick(t, start, width):
+            h, at = divmod(start, HALF)
+            nc.vector.tensor_tensor(
+                out=picked[h][:, t, at : at + width],
+                in0=x_planes[t][:].indirect(offsets[:, start // 16 : (start + width) // 16]),
+                in1=wgt_sb[h][:, at : at + width],
+                op=ALU.mult,
+            )
+
+        def weave_x(q):
+            h, at = divmod(q * CHUNK, HALF)
+            woven = keep.tile([P, CHUNK, PACK], BF16, name="x_woven%d" % q, align_bytes=64)
+            copy = nc.vector.tensor_copy if q in WEAVE_ON_VECTOR else nc.scalar.copy
+            copy(out=by_runs_woven(woven[:]), in_=by_runs_planes(picked[h][:, :, at : at + CHUNK]))
+            return woven
+
+        def c_passes(acc, pair, operand):
+            passes = []
+            for u in range(2):
+                n_cols = slice((2 * pair + u) * P, (2 * pair + u + 1) * P)
+                passes.append(
+                    dict(
+                        out=acc[:, u, :],
+                        lhsT=wx_sb[:, n_cols].bitcast(FP8X4),
+                        lhsT_scale=wx_sc[:, n_cols],
+                        rhs=operand[0][:].bitcast(FP8X4),
+                        rhs_scale=operand[1][:],
+                    )
+                )
+            return passes
+
+        def x_passes(acc, pair, q):
+            passes = []
+            for u in range(2):
+                n0 = (2 * pair + u) * P
+                for s in range(CHUNK // STRIP):
+                    cols = slice(s * STRIP, (s + 1) * STRIP)
+                    passes.append(
+                        dict(
+                            out=acc[:, u, cols],
+                            lhsT=wt_sb[:, 2 * n0 : 2 * (n0 + P)].bitcast(FP4X4),
+                            lhsT_scale=wt_sc[:, n0 : n0 + P],
+                            rhs=x_q[q][0][:, cols].bitcast(FP8X4),
+                            rhs_scale=x_q[q][1][:, cols],
+                        )
+                    )
+            return passes
+
+        accs = {}
+
+        def open_with_c(q):
+            for pair in range(2):
+                acc = psum.tile([P, 2, CHUNK], F32, name="acc", tag="acc", bufs=6)
+                accs[q, pair] = acc
+                for i, operands in enumerate(c_passes(acc, pair, c_q[q]) + c_passes(acc, pair, c_r[q])):
+                    nc.tensor.matmul_mx(**operands, start=(i == 0), stop=False)
+
+        def close_with_x(q):
+            for pair in range(2):
+                passes = x_passes(accs[q, pair], pair, q)
+                for i, operands in enumerate(passes):
+                    nc.tensor.matmul_mx(**operands, start=False, stop=(i == len(passes) - 1))
+
+        out_rows = out.rearrange("(u p) j -> p u j", p=P)
+
+        def finish(q):
+            for pair in range(2):
+                result = keep.tile([P, 2, CHUNK], F32, name="result%d_%d" % (q, pair))
+                for u in range(2):
+                    n_tile = 2 * pair + u
+                    nc.scalar.activation(
+                        out=result[:, u, :],
+                        in_=accs[q, pair][:, u, :],
+                        func=GELU,
+                        bias=bias[:, n_tile : n_tile + 1],
+                    )
+                nc.sync.dma_start(
+                    out=out_rows[:, 2 * pair : 2 * pair + 2, q * CHUNK : (q + 1) * CHUNK], in_=result[:]
+                )
+
+        for q in range(EARLY):
+            first_tier(q)
+        for q in range(EARLY):
+            left_over(q)
+        for q in range(EARLY):
+            second_tier(q)
+            open_with_c(q)
+        for t in range(PACK - 1):
+            for h in range(2):
+                pick(t, h * HALF, HALF)
+        woven_x = {}
+        for q in range(CHUNKS):
+            pick(PACK - 1, q * CHUNK, CHUNK)
+            woven_x[q] = weave_x(q)
+        for q in range(CHUNKS):
+            if q >= EARLY:
+                first_tier(q)
+            quantize(x_q[q], woven_x[q])
+            if q >= EARLY:
+                left_over(q)
+                second_tier(q)
+                open_with_c(q)
+            close_with_x(q)
+            finish(q)

@@ -23,9 +23,9 @@ CHUNK = 256
 CHUNKS = J // CHUNK
 HALF = J // 2
 STRIP = 128
-RUN = 4
-EARLY = 2
-WEAVE_ON_VECTOR = (2,)
+RUN = 2
+BACK_PAIR = (0, 1, 0, 3)
+ACC_PAIR = (1, 2, 0, 1)
 
 
 def tile_list_gelu_kernel(
@@ -34,17 +34,23 @@ def tile_list_gelu_kernel(
     nc = tc.nc
     with ExitStack() as ctx:
         keep = ctx.enter_context(tc.tile_pool(name="keep", bufs=1))
+        after_eye = ctx.enter_context(tc.tile_pool(name="after_eye", bufs=1))
+        after_c0 = ctx.enter_context(tc.tile_pool(name="after_c0", bufs=1))
+        late = ctx.enter_context(tc.tile_pool(name="late", bufs=1))
         psum = ctx.enter_context(tc.psum_pool(name="psum", bufs=1))
+
+        def bank(index, shape):
+            return psum.tile(shape, F32, name="bank%d" % index, tag="bank%d" % index)
 
         def mx_tiles(name, width):
             codes = keep.tile([P, width], U32, name=name + "_codes", align_bytes=64)
             scales = keep.tile([P, width], U8, name=name + "_scales", align_bytes=64)
             return codes, scales
 
-        def quantize(operand, woven):
+        def quantize(operand, cols, woven):
             codes, scales = operand
             nc.vector.quantize_mx(
-                out=codes[:].bitcast(FP8X4), scales=scales[:], in_=woven[:].rearrange("p j t -> p (j t)")
+                out=codes[:, cols].bitcast(FP8X4), scales=scales[:, cols], in_=woven.rearrange("p j t -> p (j t)")
             )
 
         def by_runs_planes(planes):
@@ -53,25 +59,43 @@ def tile_list_gelu_kernel(
         def by_runs_woven(woven):
             return woven.rearrange("p (c i) t -> p c t i", i=RUN)
 
+        def weave(copy, woven, planes):
+            copy(out=by_runs_woven(woven), in_=by_runs_planes(planes))
+
+        whole = slice(0, CHUNK)
+        strips = [slice(s * STRIP, (s + 1) * STRIP) for s in range(CHUNK // STRIP)]
+        picked_bytes = PACK * HALF * 4
+        woven_bytes = CHUNK * PACK * 2
+        woven_shape = [P, CHUNK, PACK]
+        strip_shape = [P, STRIP, PACK]
+
         offsets = keep.tile([P, J // 16], U16, name="offsets")
-        x_planes = [keep.tile([P, T], F32, name="x%d" % t) for t in range(PACK)]
-        wgt_sb = [keep.tile([P, HALF], F32, name="wgt%d" % h) for h in range(2)]
-        c_sb = [keep.tile([P, PACK, CHUNK], F32, name="c%d" % q) for q in range(CHUNKS)]
+        x_planes = [late.tile([P, T], F32, name="x%d" % t, tag="x%d" % t, align_bytes=64) for t in range(PACK)]
+        wgt_sb = [late.tile([P, HALF], F32, name="wgt%d" % h, tag="wgt%d" % h, align_bytes=64) for h in range(2)]
+        c_sb = [after_c0.tile([P, PACK, CHUNK], F32, name="c0", align_bytes=64, offset=picked_bytes - woven_bytes)]
+        c_sb.extend(
+            late.tile([P, PACK, CHUNK], F32, name="c%d" % q, tag="c%d" % q, align_bytes=64) for q in range(1, CHUNKS)
+        )
         wt_sb = keep.tile([P, 2 * N], U8, name="wt_sb", align_bytes=64)
         wx_sb = keep.tile([P, N], U32, name="wx_sb", align_bytes=64)
         wt_sc = keep.tile([P, N], U8, name="wt_sc", align_bytes=64)
         wx_sc = keep.tile([P, N], U8, name="wx_sc", align_bytes=64)
         bias = keep.tile([P, N // P], F32, name="bias")
-        eye = keep.tile([P, L, PACK], BF16, name="eye", align_bytes=64)
+        eye = after_eye.tile([P, L, PACK], BF16, name="eye", align_bytes=64, offset=0)
         eye_q = mx_tiles("eye", L)
 
-        nc.vector.memset(eye[:].rearrange("p m t -> p (m t)"), 0.0)
-        nc.vector.memset(wx_sc[:].bitcast(I32), 0)
-        nc.vector.memset(wt_sc[:].bitcast(I32), 0)
+        warm = keep.tile([P, 2], F32, name="warm")
+        nc.gpsimd.memset(warm[:, 0:1], 0.0)
+        nc.scalar.activation(out=warm[:, 1:2], in_=warm[:, 0:1], func=GELU)
+
+        nc.vector.memset(eye[:].rearrange("p m t -> p (m t)").bitcast(I32), 0)
+        nc.gpsimd.memset(wx_sc[:].bitcast(I32), 0)
+        nc.gpsimd.memset(wt_sc[:].bitcast(I32), 0)
         ident = keep.tile([P, P], BF16, name="ident")
         make_identity(nc, ident[:])
         for t in range(PACK):
             nc.vector.tensor_copy(out=eye[:, t * P : (t + 1) * P, t], in_=ident[:])
+        quantize(eye_q, slice(0, L), eye[:])
 
         c_rows = c.rearrange("(p t) j -> p t j", t=PACK)
         x_rows = xT.rearrange("(p t) s -> p t s", t=PACK)
@@ -85,71 +109,100 @@ def tile_list_gelu_kernel(
         def load_wgt(h):
             nc.sync.dma_start(out=wgt_sb[h][:], in_=wgt[:, h * HALF : (h + 1) * HALF])
 
-        def load_scales(plane, rows, quadrants):
-            for quad in quadrants:
+        def load_scales(plane, rows):
+            for quad in range(4):
                 nc.sync.dma_start(
                     out=plane[32 * quad : 32 * quad + 4, :].bitcast(I32),
                     in_=rows[0, 4 * quad : 4 * quad + 4, :].bitcast(I32),
                 )
 
-        for q in range(EARLY):
-            load_c(q)
-        load_wgt(0)
+        load_c(0)
+        load_c(1)
         nc.sync.dma_start(offsets[:], offs)
+        load_wgt(0)
         load_x(0)
         load_wgt(1)
-        load_scales(wx_sc, wx_scales, (0, 1))
         load_x(1)
-        nc.sync.dma_start(out=wx_sb[:].bitcast(I32), in_=wx_words[0].rearrange("p n t -> p (n t)").bitcast(I32))
-        load_scales(wx_sc, wx_scales, (2, 3))
+        load_scales(wx_sc, wx_scales)
+        load_c(2)
+        load_c(3)
         load_x(2)
-        load_scales(wt_sc, wt_scales, (0, 1))
+        nc.sync.dma_start(out=wx_sb[:].bitcast(I32), in_=wx_words[0].rearrange("p n t -> p (n t)").bitcast(I32))
+        load_scales(wt_sc, wt_scales)
         load_x(3)
-        load_scales(wt_sc, wt_scales, (2, 3))
         nc.sync.dma_start(out=wt_sb[:].bitcast(I32), in_=wt_words[0].bitcast(I32))
         with nc.allow_non_contiguous_dma(reason="one bias value for each partition"):
             nc.sync.dma_start(out=bias[:], in_=b.rearrange("(u p) -> p u", p=P))
-        for q in range(EARLY, CHUNKS):
-            load_c(q)
 
-        quantize(eye_q, eye)
-
-        c_q = [mx_tiles("cq%d" % q, CHUNK) for q in range(CHUNKS)]
+        c_q = []
+        for q in range(CHUNKS):
+            pool, at = after_eye, q * CHUNK
+            c_q.append(
+                (
+                    keep.tile([P, CHUNK], U32, name="cq%d_codes" % q, align_bytes=64),
+                    pool.tile([P, CHUNK], U8, name="cq%d_scales" % q, align_bytes=64, offset=at),
+                )
+            )
         c_r = [mx_tiles("cr%d" % q, CHUNK) for q in range(CHUNKS)]
         x_q = [mx_tiles("xq%d" % q, CHUNK) for q in range(CHUNKS)]
-        picked = [keep.tile([P, PACK, HALF], F32, name="picked%d" % h) for h in range(2)]
-        left = {}
+        c0_strips = [
+            after_eye.tile(strip_shape, BF16, name="c0_strip0", align_bytes=64, offset=CHUNKS * CHUNK),
+            keep.tile(strip_shape, BF16, name="c0_strip1", align_bytes=64),
+        ]
+        picked = [
+            after_c0.tile([P, PACK, HALF], F32, name="picked%d" % h, align_bytes=64, offset=h * (picked_bytes + CHUNK))
+            for h in range(2)
+        ]
+        tags = {"left2": "wgt0", "left3": "x_woven1"}
+        made = {}
+
+        def woven_tile(name, shape):
+            if name not in made:
+                made[name] = late.tile(shape, BF16, name=name, tag=tags.get(name, name), align_bytes=64)
+            return made[name]
+
+        def weave_c(q):
+            weave(nc.scalar.copy, woven_tile("c_woven%d" % q, woven_shape)[:], c_sb[q][:])
 
         def first_tier(q):
-            woven = keep.tile([P, CHUNK, PACK], BF16, name="c_woven%d" % q, align_bytes=64)
-            nc.scalar.copy(out=by_runs_woven(woven[:]), in_=by_runs_planes(c_sb[q][:]))
-            quantize(c_q[q], woven)
+            quantize(c_q[q], whole, made["c_woven%d" % q][:])
 
-        def left_over(q):
-            left[q] = keep.tile([P, CHUNK, PACK], BF16, name="left%d" % q, align_bytes=64)
-            for s in range(CHUNK // STRIP):
-                cols = slice(s * STRIP, (s + 1) * STRIP)
-                back = psum.tile([P, PACK, STRIP], F32, name="back", tag="back", bufs=2)
-                for t in range(PACK):
-                    rows = slice(t * P, (t + 1) * P)
-                    nc.tensor.matmul_mx(
-                        out=back[:, t, :],
-                        lhsT=eye_q[0][:, rows].bitcast(FP8X4),
-                        lhsT_scale=eye_q[1][:, rows],
-                        rhs=c_q[q][0][:, cols].bitcast(FP8X4),
-                        rhs_scale=c_q[q][1][:, cols],
-                        start=True,
-                        stop=True,
-                    )
-                nc.vector.tensor_tensor(
-                    out=by_runs_woven(left[q][:, cols, :]),
-                    in0=by_runs_planes(c_sb[q][:, :, cols]),
-                    in1=by_runs_planes(back[:]),
-                    op=ALU.subtract,
+        def left_of(q, s):
+            if q in ():
+                return woven_tile("left%d_%d" % (q, s), strip_shape)[:]
+            return woven_tile("left%d" % q, woven_shape)[:, strips[s], :]
+
+        backs = {}
+
+        def bring_back(q, s):
+            backs[q, s] = bank(2 * BACK_PAIR[q] + s, [P, PACK, STRIP])
+            for t in range(PACK):
+                rows = slice(t * P, (t + 1) * P)
+                nc.tensor.matmul_mx(
+                    out=backs[q, s][:, t, :],
+                    lhsT=eye_q[0][:, rows].bitcast(FP8X4),
+                    lhsT_scale=eye_q[1][:, rows],
+                    rhs=c_q[q][0][:, strips[s]].bitcast(FP8X4),
+                    rhs_scale=c_q[q][1][:, strips[s]],
+                    start=True,
+                    stop=True,
                 )
 
+        def left_over(q, s):
+            if (q, s) not in backs:
+                bring_back(q, s)
+            nc.vector.tensor_tensor(
+                out=by_runs_woven(left_of(q, s)),
+                in0=by_runs_planes(c_sb[q][:, :, strips[s]]),
+                in1=by_runs_planes(backs[q, s][:]),
+                op=ALU.subtract,
+            )
+
         def second_tier(q):
-            quantize(c_r[q], left[q])
+            quantize(c_r[q], whole, made["left%d" % q][:])
+
+        def second_tier_strip(q, s):
+            quantize(c_r[q], strips[s], left_of(q, s))
 
         def pick(t, start, width):
             h, at = divmod(start, HALF)
@@ -160,98 +213,144 @@ def tile_list_gelu_kernel(
                 op=ALU.mult,
             )
 
-        def weave_x(q):
+        def weave_x(copy, q, cols):
             h, at = divmod(q * CHUNK, HALF)
-            woven = keep.tile([P, CHUNK, PACK], BF16, name="x_woven%d" % q, align_bytes=64)
-            copy = nc.vector.tensor_copy if q in WEAVE_ON_VECTOR else nc.scalar.copy
-            copy(out=by_runs_woven(woven[:]), in_=by_runs_planes(picked[h][:, :, at : at + CHUNK]))
-            return woven
+            woven = woven_tile("x_woven%d" % q, woven_shape)
+            weave(copy, woven[:, cols, :], picked[h][:, :, at + cols.start : at + cols.stop])
 
-        def c_passes(acc, pair, operand):
-            passes = []
-            for u in range(2):
-                n_cols = slice((2 * pair + u) * P, (2 * pair + u + 1) * P)
-                passes.append(
-                    dict(
-                        out=acc[:, u, :],
-                        lhsT=wx_sb[:, n_cols].bitcast(FP8X4),
-                        lhsT_scale=wx_sc[:, n_cols],
-                        rhs=operand[0][:].bitcast(FP8X4),
-                        rhs_scale=operand[1][:],
-                    )
-                )
-            return passes
+        def weave_pair(copy, q, e):
+            h, at = divmod(q * CHUNK, HALF)
+            woven = woven_tile("x_woven%d" % q, woven_shape)
+            copy(
+                out=woven[:, :, 2 * e : 2 * e + 2].rearrange("p (c i) t -> p c t i", i=RUN),
+                in_=picked[h][:, 2 * e : 2 * e + 2, at : at + CHUNK].rearrange("p t (c i) -> p c t i", i=RUN),
+            )
 
-        def x_passes(acc, pair, q):
-            passes = []
-            for u in range(2):
-                n0 = (2 * pair + u) * P
-                for s in range(CHUNK // STRIP):
-                    cols = slice(s * STRIP, (s + 1) * STRIP)
-                    passes.append(
-                        dict(
-                            out=acc[:, u, cols],
-                            lhsT=wt_sb[:, 2 * n0 : 2 * (n0 + P)].bitcast(FP4X4),
-                            lhsT_scale=wt_sc[:, n0 : n0 + P],
-                            rhs=x_q[q][0][:, cols].bitcast(FP8X4),
-                            rhs_scale=x_q[q][1][:, cols],
-                        )
-                    )
-            return passes
+        def quantize_x(q):
+            quantize(x_q[q], whole, made["x_woven%d" % q][:])
 
         accs = {}
 
-        def open_with_c(q):
-            for pair in range(2):
-                acc = psum.tile([P, 2, CHUNK], F32, name="acc", tag="acc", bufs=6)
-                accs[q, pair] = acc
-                for i, operands in enumerate(c_passes(acc, pair, c_q[q]) + c_passes(acc, pair, c_r[q])):
-                    nc.tensor.matmul_mx(**operands, start=(i == 0), stop=False)
+        def add_c(q, pair, tier, cols, start=False, stop=False):
+            if start:
+                accs[q, pair] = bank(2 * ACC_PAIR[q] + pair, [P, 2, CHUNK])
+            for u in range(2):
+                n_cols = slice((2 * pair + u) * P, (2 * pair + u + 1) * P)
+                nc.tensor.matmul_mx(
+                    out=accs[q, pair][:, u, cols],
+                    lhsT=wx_sb[:, n_cols].bitcast(FP8X4),
+                    lhsT_scale=wx_sc[:, n_cols],
+                    rhs=tier[q][0][:, cols].bitcast(FP8X4),
+                    rhs_scale=tier[q][1][:, cols],
+                    start=(start and u == 0),
+                    stop=(stop and u == 1),
+                )
 
-        def close_with_x(q):
-            for pair in range(2):
-                passes = x_passes(accs[q, pair], pair, q)
-                for i, operands in enumerate(passes):
-                    nc.tensor.matmul_mx(**operands, start=False, stop=(i == len(passes) - 1))
+        def add_x(q, pair, stop):
+            for u in range(2):
+                n0 = (2 * pair + u) * P
+                for cols in strips:
+                    nc.tensor.matmul_mx(
+                        out=accs[q, pair][:, u, cols],
+                        lhsT=wt_sb[:, 2 * n0 : 2 * (n0 + P)].bitcast(FP4X4),
+                        lhsT_scale=wt_sc[:, n0 : n0 + P],
+                        rhs=x_q[q][0][:, cols].bitcast(FP8X4),
+                        rhs_scale=x_q[q][1][:, cols],
+                        start=False,
+                        stop=(stop and u == 1 and cols == strips[-1]),
+                    )
 
         out_rows = out.rearrange("(u p) j -> p u j", p=P)
 
-        def finish(q):
-            for pair in range(2):
-                result = keep.tile([P, 2, CHUNK], F32, name="result%d_%d" % (q, pair))
-                for u in range(2):
-                    n_tile = 2 * pair + u
-                    nc.scalar.activation(
-                        out=result[:, u, :],
-                        in_=accs[q, pair][:, u, :],
-                        func=GELU,
-                        bias=bias[:, n_tile : n_tile + 1],
-                    )
+        def store(q, pair):
+            result = keep.tile([P, 2, CHUNK], F32, name="result%d_%d" % (q, pair))
+            for u in range(2):
+                n_tile = 2 * pair + u
+                nc.scalar.activation(
+                    out=result[:, u, :], in_=accs[q, pair][:, u, :], func=GELU, bias=bias[:, n_tile : n_tile + 1]
+                )
+                if q == CHUNKS - 1:
+                    nc.sync.dma_start(out=out_rows[:, n_tile, q * CHUNK : (q + 1) * CHUNK], in_=result[:, u, :])
+            if q < CHUNKS - 1:
                 nc.sync.dma_start(
                     out=out_rows[:, 2 * pair : 2 * pair + 2, q * CHUNK : (q + 1) * CHUNK], in_=result[:]
                 )
 
-        for q in range(EARLY):
-            first_tier(q)
-        for q in range(EARLY):
-            left_over(q)
-        for q in range(EARLY):
-            second_tier(q)
-            open_with_c(q)
-        for t in range(PACK - 1):
-            for h in range(2):
-                pick(t, h * HALF, HALF)
-        woven_x = {}
-        for q in range(CHUNKS):
-            pick(PACK - 1, q * CHUNK, CHUNK)
-            woven_x[q] = weave_x(q)
-        for q in range(CHUNKS):
-            if q >= EARLY:
-                first_tier(q)
-            quantize(x_q[q], woven_x[q])
-            if q >= EARLY:
-                left_over(q)
-                second_tier(q)
-                open_with_c(q)
-            close_with_x(q)
-            finish(q)
+        for s, copy in enumerate((nc.vector.tensor_copy, nc.scalar.copy)):
+            weave(copy, c0_strips[s][:], c_sb[0][:, :, strips[s]])
+        for s in range(2):
+            quantize(c_q[0], strips[s], c0_strips[s][:])
+        made["c_woven1"] = after_eye.tile(woven_shape, BF16, name="c_woven1", align_bytes=64, offset=woven_bytes)
+        for s, copy in enumerate((nc.vector.tensor_copy, nc.scalar.copy)):
+            weave(copy, made["c_woven1"][:, strips[s], :], c_sb[1][:, :, strips[s]])
+        weave_c(2)
+        weave_c(3)
+        first_tier(1)
+        left_over(0, 1)
+        left_over(0, 0)
+        left_over(1, 0)
+        second_tier(0)
+        left_over(1, 1)
+        pick(0, 0, HALF)
+        second_tier(1)
+        pick(0, HALF, HALF)
+        pick(1, 0, HALF)
+        weave_pair(nc.scalar.copy, 0, 0)
+        weave_pair(nc.scalar.copy, 1, 0)
+        pick(1, HALF, HALF)
+        weave_pair(nc.scalar.copy, 2, 0)
+        weave_pair(nc.scalar.copy, 3, 0)
+        first_tier(2)
+        first_tier(3)
+        bring_back(2, 0)
+        bring_back(2, 1)
+        bring_back(3, 0)
+        bring_back(3, 1)
+        for pair in range(2):
+            add_c(0, pair, c_q, whole, start=True)
+            add_c(0, pair, c_r, whole)
+        for pair in range(2):
+            add_c(1, pair, c_q, whole, start=True)
+            add_c(1, pair, c_r, whole)
+        pick(2, 0, HALF)
+        pick(2, HALF, HALF)
+        pick(PACK - 1, 0 * CHUNK, CHUNK)
+        weave_pair(nc.scalar.copy, 0, 1)
+        pick(PACK - 1, 1 * CHUNK, CHUNK)
+        weave_pair(nc.scalar.copy, 1, 1)
+        pick(PACK - 1, 2 * CHUNK, CHUNK)
+        weave_pair(nc.scalar.copy, 2, 1)
+        quantize_x(0)
+        for pair in range(2):
+            add_x(0, pair, stop=True)
+            store(0, pair)
+        left_over(2, 0)
+        quantize_x(1)
+        for pair in range(2):
+            add_x(1, pair, stop=True)
+            store(1, pair)
+        left_over(2, 1)
+        pick(PACK - 1, 3 * CHUNK, CHUNK)
+        second_tier(2)
+        for pair in range(2):
+            add_c(2, pair, c_q, whole, start=True)
+            add_c(2, pair, c_r, whole)
+        quantize_x(2)
+        for pair in range(2):
+            add_x(2, pair, stop=True)
+            store(2, pair)
+        weave_pair(nc.vector.tensor_copy, 3, 1)
+        left_over(3, 0)
+        for pair in range(2):
+            add_c(3, pair, c_q, whole, start=True)
+        quantize_x(3)
+        for pair in range(2):
+            add_x(3, pair, stop=False)
+        left_over(3, 1)
+        second_tier_strip(3, 0)
+        second_tier_strip(3, 1)
+        for pair in range(2):
+            add_c(3, pair, c_r, strips[0])
+        for pair in range(2):
+            add_c(3, pair, c_r, strips[1], stop=True)
+            store(3, pair)

@@ -19,13 +19,12 @@ GELU = mybir.ActivationFunctionType.Gelu_apprx_tanh
 
 P = 128
 PACK = 4
-CHUNK = 256
+QUAD = 32
+STRIP = 128
+CHUNK = 2 * STRIP
 CHUNKS = J // CHUNK
 HALF = J // 2
-STRIP = 128
 RUN = 2
-BACK_PAIR = (0, 1, 0, 3)
-ACC_PAIR = (1, 2, 0, 1)
 
 
 def tile_list_gelu_kernel(
@@ -34,24 +33,21 @@ def tile_list_gelu_kernel(
     nc = tc.nc
     with ExitStack() as ctx:
         keep = ctx.enter_context(tc.tile_pool(name="keep", bufs=1))
-        after_eye = ctx.enter_context(tc.tile_pool(name="after_eye", bufs=1))
-        after_c0 = ctx.enter_context(tc.tile_pool(name="after_c0", bufs=1))
-        late = ctx.enter_context(tc.tile_pool(name="late", bufs=1))
+        laid = ctx.enter_context(tc.tile_pool(name="laid", bufs=1))
         psum = ctx.enter_context(tc.psum_pool(name="psum", bufs=1))
+
+        laid_at = {"eye": 0, "cw0_0": 0, "cw1": 1024, "cq0_scales": 3072, "cw2": 4032, "c0": 6144, "cq2_scales": 6144, "picked01": 10304, "c2": 18432, "left2": 28672, "host3": 28672}
+
+        def tile(name, shape, dtype, tag=None):
+            if name in laid_at:
+                return laid.tile(shape, dtype, name=name, align_bytes=64, offset=laid_at[name])
+            return keep.tile(shape, dtype, name=name, tag=tag or name, align_bytes=64)
 
         def bank(index, shape):
             return psum.tile(shape, F32, name="bank%d" % index, tag="bank%d" % index)
 
         def mx_tiles(name, width):
-            codes = keep.tile([P, width], U32, name=name + "_codes", align_bytes=64)
-            scales = keep.tile([P, width], U8, name=name + "_scales", align_bytes=64)
-            return codes, scales
-
-        def quantize(operand, cols, woven):
-            codes, scales = operand
-            nc.vector.quantize_mx(
-                out=codes[:, cols].bitcast(FP8X4), scales=scales[:, cols], in_=woven.rearrange("p j t -> p (j t)")
-            )
+            return tile(name + "_codes", [P, width], U32), tile(name + "_scales", [P, width], U8)
 
         def by_runs_planes(planes):
             return planes.rearrange("p t (c i) -> p c t i", i=RUN)
@@ -59,298 +55,273 @@ def tile_list_gelu_kernel(
         def by_runs_woven(woven):
             return woven.rearrange("p (c i) t -> p c t i", i=RUN)
 
-        def weave(copy, woven, planes):
-            copy(out=by_runs_woven(woven), in_=by_runs_planes(planes))
-
-        whole = slice(0, CHUNK)
-        strips = [slice(s * STRIP, (s + 1) * STRIP) for s in range(CHUNK // STRIP)]
-        picked_bytes = PACK * HALF * 4
-        woven_bytes = CHUNK * PACK * 2
-        woven_shape = [P, CHUNK, PACK]
-        strip_shape = [P, STRIP, PACK]
+        def places(first, count=1):
+            return slice(first * STRIP, (first + count) * STRIP)
 
         offsets = keep.tile([P, J // 16], U16, name="offsets")
-        x_planes = [late.tile([P, T], F32, name="x%d" % t, tag="x%d" % t, align_bytes=64) for t in range(PACK)]
-        wgt_sb = [late.tile([P, HALF], F32, name="wgt%d" % h, tag="wgt%d" % h, align_bytes=64) for h in range(2)]
-        c_sb = [after_c0.tile([P, PACK, CHUNK], F32, name="c0", align_bytes=64, offset=picked_bytes - woven_bytes)]
-        c_sb.extend(
-            late.tile([P, PACK, CHUNK], F32, name="c%d" % q, tag="c%d" % q, align_bytes=64) for q in range(1, CHUNKS)
-        )
-        wt_sb = keep.tile([P, 2 * N], U8, name="wt_sb", align_bytes=64)
-        wx_sb = keep.tile([P, N], U32, name="wx_sb", align_bytes=64)
-        wt_sc = keep.tile([P, N], U8, name="wt_sc", align_bytes=64)
-        wx_sc = keep.tile([P, N], U8, name="wx_sc", align_bytes=64)
-        bias = keep.tile([P, N // P], F32, name="bias")
-        eye = after_eye.tile([P, L, PACK], BF16, name="eye", align_bytes=64, offset=0)
-        eye_q = mx_tiles("eye", L)
+        x_planes = [tile("x%d" % t, [P, T], F32) for t in range(PACK)]
+        wt_sb = tile("wt_sb", [P, 2 * N], U8)
+        wx_sb = tile("wx_sb", [P, N], U32)
+        wt_sc = tile("wt_sc", [P, N], U8)
+        wx_sc = tile("wx_sc", [P, N], U8)
+        bias = tile("bias", [P, N // P], F32)
 
-        warm = keep.tile([P, 2], F32, name="warm")
-        nc.gpsimd.memset(warm[:, 0:1], 0.0)
+        ident = tile("ident", [P, P], BF16)
+        make_identity(nc, ident[:])
+        warm = tile("warm", [P, 2], F32)
+        nc.vector.memset(warm[:, 0:1], 0.0)
         nc.scalar.activation(out=warm[:, 1:2], in_=warm[:, 0:1], func=GELU)
 
+        eye = tile("eye", [P, L, PACK], BF16)
+        eye_q = mx_tiles("eye", L)
         nc.vector.memset(eye[:].rearrange("p m t -> p (m t)").bitcast(I32), 0)
-        nc.gpsimd.memset(wx_sc[:].bitcast(I32), 0)
-        nc.gpsimd.memset(wt_sc[:].bitcast(I32), 0)
-        ident = keep.tile([P, P], BF16, name="ident")
-        make_identity(nc, ident[:])
+        nc.vector.memset(wx_sc[:].bitcast(I32), 0)
+        nc.vector.memset(wt_sc[:].bitcast(I32), 0)
         for t in range(PACK):
-            nc.vector.tensor_copy(out=eye[:, t * P : (t + 1) * P, t], in_=ident[:])
-        quantize(eye_q, slice(0, L), eye[:])
+            nc.vector.tensor_copy(out=eye[:, places(t), t], in_=ident[:])
+        nc.vector.quantize_mx(
+            out=eye_q[0][:].bitcast(FP8X4), scales=eye_q[1][:], in_=eye[:].rearrange("p m t -> p (m t)")
+        )
 
         c_rows = c.rearrange("(p t) j -> p t j", t=PACK)
         x_rows = xT.rearrange("(p t) s -> p t s", t=PACK)
+        out_rows = out.rearrange("(u p) j -> p u j", p=P)
+
+        def load_scales(plane, rows):
+            for quad in range(P // QUAD):
+                nc.sync.dma_start(
+                    out=plane[QUAD * quad : QUAD * quad + 4, :].bitcast(I32),
+                    in_=rows[0, 4 * quad : 4 * quad + 4, :].bitcast(I32),
+                )
+
+        def load_bias():
+            with nc.allow_non_contiguous_dma(reason="one bias value for each partition"):
+                nc.sync.dma_start(out=bias[:], in_=b.rearrange("(u p) -> p u", p=P))
+
+        tags = {}
+        lodged = {("left", 1): (2, 0), ("xw", 0): (3, 1), ("cw", 3): (3, 3)}
+        made = {}
+
+        def once(name, shape, dtype):
+            if name not in made:
+                made[name] = tile(name, shape, dtype, tags.get(name))
+            return made[name]
+
+        def c_tile(q):
+            return once("c%d" % q, [P, PACK, CHUNK], F32)
+
+        def host(q):
+            return once("host%d" % q, [P, 6 * CHUNK], F32)
+
+        def picked(q):
+            if q < 2:
+                return once("picked01", [P, PACK, HALF], F32)[:], q * CHUNK
+            return host(q)[:, 0 : PACK * CHUNK].rearrange("p (t j) -> p t j", t=PACK), 0
+
+        def woven(name, q):
+            if (name, q) in lodged:
+                where, first = lodged[name, q]
+                words = host(where)[:, first * CHUNK : (first + 2) * CHUNK]
+                return words.bitcast(BF16).rearrange("p (j t) -> p j t", t=PACK)
+            return once("%s%d" % (name, q), [P, CHUNK, PACK], BF16)[:]
+
+        def woven_part(name, q, cols):
+            if (name, q) == ("cw", 0):
+                return once("cw0_%d" % (cols.start // STRIP), [P, STRIP, PACK], BF16)[:]
+            return woven(name, q)[:, cols, :]
 
         def load_c(q):
-            nc.sync.dma_start(out=c_sb[q][:], in_=c_rows[:, :, q * CHUNK : (q + 1) * CHUNK])
+            nc.sync.dma_start(out=c_tile(q)[:], in_=c_rows[:, :, places(2 * q, 2)])
 
         def load_x(t):
             nc.sync.dma_start(out=x_planes[t][:], in_=x_rows[:, t, :])
 
-        def load_wgt(h):
-            nc.sync.dma_start(out=wgt_sb[h][:], in_=wgt[:, h * HALF : (h + 1) * HALF])
+        wgt_sb = host(2)[:, 2 * CHUNK :]
 
-        def load_scales(plane, rows):
-            for quad in range(4):
-                nc.sync.dma_start(
-                    out=plane[32 * quad : 32 * quad + 4, :].bitcast(I32),
-                    in_=rows[0, 4 * quad : 4 * quad + 4, :].bitcast(I32),
-                )
+        def load_wx():
+            nc.sync.dma_start(out=wx_sb[:].bitcast(I32), in_=wx_words[0].rearrange("p n t -> p (n t)").bitcast(I32))
+
+        def load_wt():
+            nc.sync.dma_start(out=wt_sb[:].bitcast(I32), in_=wt_words[0].bitcast(I32))
 
         load_c(0)
         load_c(1)
+        load_c(2)
         nc.sync.dma_start(offsets[:], offs)
-        load_wgt(0)
+        nc.sync.dma_start(out=wgt_sb, in_=wgt)
         load_x(0)
-        load_wgt(1)
         load_x(1)
         load_scales(wx_sc, wx_scales)
-        load_c(2)
-        load_c(3)
         load_x(2)
-        nc.sync.dma_start(out=wx_sb[:].bitcast(I32), in_=wx_words[0].rearrange("p n t -> p (n t)").bitcast(I32))
+        load_wx()
         load_scales(wt_sc, wt_scales)
         load_x(3)
-        nc.sync.dma_start(out=wt_sb[:].bitcast(I32), in_=wt_words[0].bitcast(I32))
-        with nc.allow_non_contiguous_dma(reason="one bias value for each partition"):
-            nc.sync.dma_start(out=bias[:], in_=b.rearrange("(u p) -> p u", p=P))
+        load_wt()
+        load_c(3)
+        load_bias()
 
-        c_q = []
-        for q in range(CHUNKS):
-            pool, at = after_eye, q * CHUNK
-            c_q.append(
-                (
-                    keep.tile([P, CHUNK], U32, name="cq%d_codes" % q, align_bytes=64),
-                    pool.tile([P, CHUNK], U8, name="cq%d_scales" % q, align_bytes=64, offset=at),
-                )
+        whole = places(0, 2)
+        quantised = {name: [mx_tiles("%s%d" % (name, q), CHUNK) for q in range(CHUNKS)] for name in ("cq", "cr", "xq")}
+
+        def quantize(name, source, q, cols):
+            codes, scales = quantised[name][q]
+            nc.vector.quantize_mx(
+                out=codes[:, cols].bitcast(FP8X4),
+                scales=scales[:, cols],
+                in_=woven_part(source, q, cols).rearrange("p j t -> p (j t)"),
             )
-        c_r = [mx_tiles("cr%d" % q, CHUNK) for q in range(CHUNKS)]
-        x_q = [mx_tiles("xq%d" % q, CHUNK) for q in range(CHUNKS)]
-        c0_strips = [
-            after_eye.tile(strip_shape, BF16, name="c0_strip0", align_bytes=64, offset=CHUNKS * CHUNK),
-            keep.tile(strip_shape, BF16, name="c0_strip1", align_bytes=64),
-        ]
-        picked = [
-            after_c0.tile([P, PACK, HALF], F32, name="picked%d" % h, align_bytes=64, offset=h * (picked_bytes + CHUNK))
-            for h in range(2)
-        ]
-        tags = {"left2": "wgt0", "left3": "x_woven1"}
-        made = {}
 
-        def woven_tile(name, shape):
-            if name not in made:
-                made[name] = late.tile(shape, BF16, name=name, tag=tags.get(name, name), align_bytes=64)
-            return made[name]
 
-        def weave_c(q):
-            weave(nc.scalar.copy, woven_tile("c_woven%d" % q, woven_shape)[:], c_sb[q][:])
-
-        def first_tier(q):
-            quantize(c_q[q], whole, made["c_woven%d" % q][:])
-
-        def left_of(q, s):
-            if q in ():
-                return woven_tile("left%d_%d" % (q, s), strip_shape)[:]
-            return woven_tile("left%d" % q, woven_shape)[:, strips[s], :]
+        def weave_c(copy, q, cols):
+            copy(out=by_runs_woven(woven_part("cw", q, cols)), in_=by_runs_planes(c_tile(q)[:, :, cols]))
 
         backs = {}
 
         def bring_back(q, s):
-            backs[q, s] = bank(2 * BACK_PAIR[q] + s, [P, PACK, STRIP])
+            backs[q, s] = bank(2 * q + s, [P, PACK, STRIP])
+            codes, scales = quantised["cq"][q]
             for t in range(PACK):
-                rows = slice(t * P, (t + 1) * P)
                 nc.tensor.matmul_mx(
                     out=backs[q, s][:, t, :],
-                    lhsT=eye_q[0][:, rows].bitcast(FP8X4),
-                    lhsT_scale=eye_q[1][:, rows],
-                    rhs=c_q[q][0][:, strips[s]].bitcast(FP8X4),
-                    rhs_scale=c_q[q][1][:, strips[s]],
+                    lhsT=eye_q[0][:, places(t)].bitcast(FP8X4),
+                    lhsT_scale=eye_q[1][:, places(t)],
+                    rhs=codes[:, places(s)].bitcast(FP8X4),
+                    rhs_scale=scales[:, places(s)],
                     start=True,
                     stop=True,
                 )
 
+        def first_tier(q, s=None):
+            quantize("cq", "cw", q, whole if s is None else places(s))
+            for strip in range(2) if s is None else (s,):
+                bring_back(q, strip)
+
         def left_over(q, s):
-            if (q, s) not in backs:
-                bring_back(q, s)
             nc.vector.tensor_tensor(
-                out=by_runs_woven(left_of(q, s)),
-                in0=by_runs_planes(c_sb[q][:, :, strips[s]]),
+                out=by_runs_woven(woven("left", q)[:, places(s), :]),
+                in0=by_runs_planes(c_tile(q)[:, :, places(s)]),
                 in1=by_runs_planes(backs[q, s][:]),
                 op=ALU.subtract,
             )
 
-        def second_tier(q):
-            quantize(c_r[q], whole, made["left%d" % q][:])
-
-        def second_tier_strip(q, s):
-            quantize(c_r[q], strips[s], left_of(q, s))
-
-        def pick(t, start, width):
-            h, at = divmod(start, HALF)
+        def pick(t, q, count=1):
+            target, at = picked(q)
+            start, width = q * CHUNK, count * CHUNK
             nc.vector.tensor_tensor(
-                out=picked[h][:, t, at : at + width],
+                out=target[:, t, at : at + width],
                 in0=x_planes[t][:].indirect(offsets[:, start // 16 : (start + width) // 16]),
-                in1=wgt_sb[h][:, at : at + width],
+                in1=wgt_sb[:, start : start + width],
                 op=ALU.mult,
             )
 
-        def weave_x(copy, q, cols):
-            h, at = divmod(q * CHUNK, HALF)
-            woven = woven_tile("x_woven%d" % q, woven_shape)
-            weave(copy, woven[:, cols, :], picked[h][:, :, at + cols.start : at + cols.stop])
+        def pick_plane(t):
+            pick(t, 0, 2)
+            pick(t, 2)
+            pick(t, 3)
 
-        def weave_pair(copy, q, e):
-            h, at = divmod(q * CHUNK, HALF)
-            woven = woven_tile("x_woven%d" % q, woven_shape)
-            copy(
-                out=woven[:, :, 2 * e : 2 * e + 2].rearrange("p (c i) t -> p c t i", i=RUN),
-                in_=picked[h][:, 2 * e : 2 * e + 2, at : at + CHUNK].rearrange("p t (c i) -> p c t i", i=RUN),
-            )
-
-        def quantize_x(q):
-            quantize(x_q[q], whole, made["x_woven%d" % q][:])
+        def weave_x(copy, q):
+            source, at = picked(q)
+            copy(out=by_runs_woven(woven("xw", q)), in_=by_runs_planes(source[:, :, at : at + CHUNK]))
 
         accs = {}
 
-        def add_c(q, pair, tier, cols, start=False, stop=False):
+        def project(name, q, s, start=False, stop=False):
+            last = q == CHUNKS - 1
+            tiles = range(PACK) if last else range(2 * s, 2 * s + 2)
+            cols = places(s) if last else whole
             if start:
-                accs[q, pair] = bank(2 * ACC_PAIR[q] + pair, [P, 2, CHUNK])
-            for u in range(2):
-                n_cols = slice((2 * pair + u) * P, (2 * pair + u + 1) * P)
+                accs[q, s] = bank(2 * (q % (CHUNKS - 1)) + s, [P, PACK, STRIP] if last else [P, 2, CHUNK])
+            codes, scales = quantised[name][q]
+            for i, u in enumerate(tiles):
+                if name == "xq":
+                    words, plane = wt_sb[:, 2 * u * P : 2 * (u + 1) * P].bitcast(FP4X4), wt_sc
+                else:
+                    words, plane = wx_sb[:, places(u)].bitcast(FP8X4), wx_sc
                 nc.tensor.matmul_mx(
-                    out=accs[q, pair][:, u, cols],
-                    lhsT=wx_sb[:, n_cols].bitcast(FP8X4),
-                    lhsT_scale=wx_sc[:, n_cols],
-                    rhs=tier[q][0][:, cols].bitcast(FP8X4),
-                    rhs_scale=tier[q][1][:, cols],
-                    start=(start and u == 0),
-                    stop=(stop and u == 1),
+                    out=accs[q, s][:, i, :],
+                    lhsT=words,
+                    lhsT_scale=plane[:, places(u)],
+                    rhs=codes[:, cols].bitcast(FP8X4),
+                    rhs_scale=scales[:, cols],
+                    start=(start and i == 0),
+                    stop=(stop and i == len(tiles) - 1),
                 )
 
-        def add_x(q, pair, stop):
-            for u in range(2):
-                n0 = (2 * pair + u) * P
-                for cols in strips:
-                    nc.tensor.matmul_mx(
-                        out=accs[q, pair][:, u, cols],
-                        lhsT=wt_sb[:, 2 * n0 : 2 * (n0 + P)].bitcast(FP4X4),
-                        lhsT_scale=wt_sc[:, n0 : n0 + P],
-                        rhs=x_q[q][0][:, cols].bitcast(FP8X4),
-                        rhs_scale=x_q[q][1][:, cols],
-                        start=False,
-                        stop=(stop and u == 1 and cols == strips[-1]),
-                    )
+        def finish(q, s):
+            last = q == CHUNKS - 1
+            tiles = range(PACK) if last else range(2 * s, 2 * s + 2)
+            cols = places(2 * q + s) if last else places(2 * q, 2)
+            result = tile("result%d_%d" % (q, s), [P, PACK, STRIP] if last else [P, 2, CHUNK], F32)
+            for i, u in enumerate(tiles):
+                nc.scalar.activation(out=result[:, i, :], in_=accs[q, s][:, i, :], func=GELU, bias=bias[:, u : u + 1])
+                if i % 2 == 1:
+                    nc.sync.dma_start(out=out_rows[:, u - 1 : u + 1, cols], in_=result[:, i - 1 : i + 1, :])
 
-        out_rows = out.rearrange("(u p) j -> p u j", p=P)
-
-        def store(q, pair):
-            result = keep.tile([P, 2, CHUNK], F32, name="result%d_%d" % (q, pair))
-            for u in range(2):
-                n_tile = 2 * pair + u
-                nc.scalar.activation(
-                    out=result[:, u, :], in_=accs[q, pair][:, u, :], func=GELU, bias=bias[:, n_tile : n_tile + 1]
-                )
-                if q == CHUNKS - 1:
-                    nc.sync.dma_start(out=out_rows[:, n_tile, q * CHUNK : (q + 1) * CHUNK], in_=result[:, u, :])
-            if q < CHUNKS - 1:
-                nc.sync.dma_start(
-                    out=out_rows[:, 2 * pair : 2 * pair + 2, q * CHUNK : (q + 1) * CHUNK], in_=result[:]
-                )
-
-        for s, copy in enumerate((nc.vector.tensor_copy, nc.scalar.copy)):
-            weave(copy, c0_strips[s][:], c_sb[0][:, :, strips[s]])
-        for s in range(2):
-            quantize(c_q[0], strips[s], c0_strips[s][:])
-        made["c_woven1"] = after_eye.tile(woven_shape, BF16, name="c_woven1", align_bytes=64, offset=woven_bytes)
-        for s, copy in enumerate((nc.vector.tensor_copy, nc.scalar.copy)):
-            weave(copy, made["c_woven1"][:, strips[s], :], c_sb[1][:, :, strips[s]])
-        weave_c(2)
-        weave_c(3)
+        on_vector, on_scalar = nc.vector.tensor_copy, nc.scalar.copy
+        weave_c(on_vector, 0, places(0))
+        weave_c(on_scalar, 0, places(1))
+        first_tier(0, 0)
+        first_tier(0, 1)
+        weave_c(on_vector, 1, places(0))
+        weave_c(on_scalar, 1, places(1))
+        weave_c(on_scalar, 2, whole)
         first_tier(1)
         left_over(0, 1)
         left_over(0, 0)
         left_over(1, 0)
-        second_tier(0)
-        left_over(1, 1)
-        pick(0, 0, HALF)
-        second_tier(1)
-        pick(0, HALF, HALF)
-        pick(1, 0, HALF)
-        weave_pair(nc.scalar.copy, 0, 0)
-        weave_pair(nc.scalar.copy, 1, 0)
-        pick(1, HALF, HALF)
-        weave_pair(nc.scalar.copy, 2, 0)
-        weave_pair(nc.scalar.copy, 3, 0)
         first_tier(2)
-        first_tier(3)
-        bring_back(2, 0)
-        bring_back(2, 1)
-        bring_back(3, 0)
-        bring_back(3, 1)
-        for pair in range(2):
-            add_c(0, pair, c_q, whole, start=True)
-            add_c(0, pair, c_r, whole)
-        for pair in range(2):
-            add_c(1, pair, c_q, whole, start=True)
-            add_c(1, pair, c_r, whole)
-        pick(2, 0, HALF)
-        pick(2, HALF, HALF)
-        pick(PACK - 1, 0 * CHUNK, CHUNK)
-        weave_pair(nc.scalar.copy, 0, 1)
-        pick(PACK - 1, 1 * CHUNK, CHUNK)
-        weave_pair(nc.scalar.copy, 1, 1)
-        pick(PACK - 1, 2 * CHUNK, CHUNK)
-        weave_pair(nc.scalar.copy, 2, 1)
-        quantize_x(0)
-        for pair in range(2):
-            add_x(0, pair, stop=True)
-            store(0, pair)
+        left_over(1, 1)
+        quantize("cr", "left", 0, whole)
         left_over(2, 0)
-        quantize_x(1)
-        for pair in range(2):
-            add_x(1, pair, stop=True)
-            store(1, pair)
         left_over(2, 1)
-        pick(PACK - 1, 3 * CHUNK, CHUNK)
-        second_tier(2)
-        for pair in range(2):
-            add_c(2, pair, c_q, whole, start=True)
-            add_c(2, pair, c_r, whole)
-        quantize_x(2)
-        for pair in range(2):
-            add_x(2, pair, stop=True)
-            store(2, pair)
-        weave_pair(nc.vector.tensor_copy, 3, 1)
+        quantize("cr", "left", 1, whole)
+        pick(0, 0, 2)
+        quantize("cr", "left", 2, whole)
+        pick(0, 2)
+        pick(0, 3)
+        pick(1, 0, 2)
+        pick(1, 2)
+        pick(2, 0, 2)
+        for q in range(3):
+            for s in range(2):
+                project("cq", q, s, start=True)
+                project("cr", q, s)
+        pick(3, 0)
+        weave_x(on_scalar, 0)
+        pick(3, 1)
+        weave_x(on_scalar, 1)
+        weave_c(on_scalar, 3, whole)
+        pick(2, 2)
+        pick(3, 2)
+        quantize("xq", "xw", 0, whole)
+        for s in range(2):
+            project("xq", 0, s, stop=True)
+        weave_x(on_scalar, 2)
+        finish(0, 0)
+        finish(0, 1)
+        pick(1, 3)
+        quantize("xq", "xw", 1, whole)
+        for s in range(2):
+            project("xq", 1, s, stop=True)
+            finish(1, s)
+        pick(2, 3)
+        first_tier(3)
+        for s in range(2):
+            project("cq", 3, s, start=True)
+        pick(3, 3)
+        quantize("xq", "xw", 2, whole)
+        for s in range(2):
+            project("xq", 2, s, stop=True)
+            finish(2, s)
         left_over(3, 0)
-        for pair in range(2):
-            add_c(3, pair, c_q, whole, start=True)
-        quantize_x(3)
-        for pair in range(2):
-            add_x(3, pair, stop=False)
+        weave_x(on_vector, 3)
+        quantize("cr", "left", 3, places(0))
+        project("cr", 3, 0)
+        quantize("xq", "xw", 3, whole)
+        project("xq", 3, 0, stop=True)
+        finish(3, 0)
         left_over(3, 1)
-        second_tier_strip(3, 0)
-        second_tier_strip(3, 1)
-        for pair in range(2):
-            add_c(3, pair, c_r, strips[0])
-        for pair in range(2):
-            add_c(3, pair, c_r, strips[1], stop=True)
-            store(3, pair)
+        project("xq", 3, 1)
+        quantize("cr", "left", 3, places(1))
+        project("cr", 3, 1, stop=True)
+        finish(3, 1)

@@ -25,6 +25,7 @@ CHUNK = 2 * STRIP
 CHUNKS = J // CHUNK
 HALF = J // 2
 RUN = 2
+GROUP = 16
 
 
 def tile_list_gelu_kernel(
@@ -36,7 +37,7 @@ def tile_list_gelu_kernel(
         laid = ctx.enter_context(tc.tile_pool(name="laid", bufs=1))
         psum = ctx.enter_context(tc.psum_pool(name="psum", bufs=1))
 
-        laid_at = {"eye": 0, "cw0_0": 0, "cw1": 1024, "cq0_scales": 3072, "cw2": 4032, "c0": 6144, "cq2_scales": 6144, "picked01": 10304, "c2": 18432, "left2": 28672, "host3": 28672}
+        laid_at = {"eye": 0, "cw0_0": 0, "cw1": 1024, "cq0_scales": 3072, "cw2": 4032, "c0": 8192, "cq2_scales": 8192, "c2": 12544, "front": 16576}
 
         def tile(name, shape, dtype, tag=None):
             if name in laid_at:
@@ -66,22 +67,20 @@ def tile_list_gelu_kernel(
         wx_sc = tile("wx_sc", [P, N], U8)
         bias = tile("bias", [P, N // P], F32)
 
-        ident = tile("ident", [P, P], BF16)
+        ident = tile("ident", [P, P], F32)
         make_identity(nc, ident[:])
         warm = tile("warm", [P, 2], F32)
         nc.vector.memset(warm[:, 0:1], 0.0)
         nc.scalar.activation(out=warm[:, 1:2], in_=warm[:, 0:1], func=GELU)
 
-        eye = tile("eye", [P, L, PACK], BF16)
+        eye = tile("eye", [P, PACK * (L + 2)], BF16)
         eye_q = mx_tiles("eye", L)
-        nc.vector.memset(eye[:].rearrange("p m t -> p (m t)").bitcast(I32), 0)
+        nc.vector.memset(eye[:].bitcast(I32), 0)
         nc.vector.memset(wx_sc[:].bitcast(I32), 0)
         nc.vector.memset(wt_sc[:].bitcast(I32), 0)
-        for t in range(PACK):
-            nc.vector.tensor_copy(out=eye[:, places(t), t], in_=ident[:])
-        nc.vector.quantize_mx(
-            out=eye_q[0][:].bitcast(FP8X4), scales=eye_q[1][:], in_=eye[:].rearrange("p m t -> p (m t)")
-        )
+        slots = eye[:, 0 : PACK * (L + 1)].rearrange("p (t r) -> p t r", t=PACK)[:, :, 0:L:PACK]
+        nc.vector.tensor_copy(out=slots, in_=ident[:].unsqueeze(1).to_broadcast([P, PACK, P]))
+        nc.vector.quantize_mx(out=eye_q[0][:].bitcast(FP8X4), scales=eye_q[1][:], in_=eye[:, 0 : PACK * L])
 
         c_rows = c.rearrange("(p t) j -> p t j", t=PACK)
         x_rows = xT.rearrange("(p t) s -> p t s", t=PACK)
@@ -99,7 +98,6 @@ def tile_list_gelu_kernel(
                 nc.sync.dma_start(out=bias[:], in_=b.rearrange("(u p) -> p u", p=P))
 
         tags = {}
-        lodged = {("left", 1): (2, 0), ("xw", 0): (3, 1), ("cw", 3): (3, 3)}
         made = {}
 
         def once(name, shape, dtype):
@@ -110,24 +108,33 @@ def tile_list_gelu_kernel(
         def c_tile(q):
             return once("c%d" % q, [P, PACK, CHUNK], F32)
 
-        def host(q):
-            return once("host%d" % q, [P, 6 * CHUNK], F32)
+        def front():
+            return once("front", [P, CHUNK + PACK * HALF], F32)
+
+        def third():
+            return once("third", [P, (PACK + 1) * CHUNK], F32)
+
+        def as_planes(words):
+            return words.rearrange("p (t j) -> p t j", t=PACK)
+
+        def as_woven(words):
+            return words.bitcast(BF16).rearrange("p (j t) -> p j t", t=PACK)
 
         def picked(q):
             if q < 2:
-                return once("picked01", [P, PACK, HALF], F32)[:], q * CHUNK
-            return host(q)[:, 0 : PACK * CHUNK].rearrange("p (t j) -> p t j", t=PACK), 0
+                return as_planes(front()[:, CHUNK:]), q * CHUNK
+            return as_planes(third()[:, CHUNK:] if q == 2 else front()[:, 0 : PACK * CHUNK]), 0
 
         def woven(name, q):
-            if (name, q) in lodged:
-                where, first = lodged[name, q]
-                words = host(where)[:, first * CHUNK : (first + 2) * CHUNK]
-                return words.bitcast(BF16).rearrange("p (j t) -> p j t", t=PACK)
+            if (name, q) == ("left", 1):
+                return as_woven(third()[:, 0 : 2 * CHUNK])
             return once("%s%d" % (name, q), [P, CHUNK, PACK], BF16)[:]
 
         def woven_part(name, q, cols):
             if (name, q) == ("cw", 0):
                 return once("cw0_%d" % (cols.start // STRIP), [P, STRIP, PACK], BF16)[:]
+            if (name, q) == ("left", CHUNKS - 1):
+                return as_woven(front()[:, PACK * HALF :] if cols.start == 0 else third()[:, CHUNK : 2 * CHUNK])
             return woven(name, q)[:, cols, :]
 
         def load_c(q):
@@ -136,7 +143,33 @@ def tile_list_gelu_kernel(
         def load_x(t):
             nc.sync.dma_start(out=x_planes[t][:], in_=x_rows[:, t, :])
 
-        wgt_sb = host(2)[:, 2 * CHUNK :]
+        wgt_sb = [third()[:, 2 * CHUNK : 4 * CHUNK], tile("wgt1", [P, HALF], F32)[:]]
+
+        wgt_rows = tile("wgt_rows", [P, P], F32)
+
+        def load_wgt():
+            rows = wgt.rearrange("(g r) (b j) -> (r b) g j", r=GROUP, j=P)
+            nc.sync.dma_start(out=wgt_rows[:], in_=rows[0:GROUP])
+
+        turned = {}
+
+        def spread_wgt(h):
+            if not turned:
+                turned["rows"] = bank(1, [P, GROUP, P // GROUP])
+                nc.tensor.transpose(turned["rows"][:].rearrange("p b g -> p (b g)"), wgt_rows[:], ident[:])
+            blocks = HALF // P
+            spread = tile("spread%d" % h, [P, blocks, P // GROUP, GROUP], F32)
+            columns = turned["rows"][:, h * blocks : (h + 1) * blocks, :]
+            nc.scalar.copy(out=spread[:], in_=columns.unsqueeze(3).to_broadcast([P, blocks, P // GROUP, GROUP]))
+            turned[h] = spread
+
+        def turn_wgt(h):
+            back = bank(3 + h, [P, HALF])
+            for block in range(HALF // P):
+                nc.tensor.transpose(
+                    back[:, places(block)], turned[h][:, block, :, :].rearrange("p g r -> p (g r)"), ident[:]
+                )
+            nc.scalar.copy(out=wgt_sb[h], in_=back[:])
 
         def load_wx():
             nc.sync.dma_start(out=wx_sb[:].bitcast(I32), in_=wx_words[0].rearrange("p n t -> p (n t)").bitcast(I32))
@@ -147,17 +180,17 @@ def tile_list_gelu_kernel(
         load_c(0)
         load_c(1)
         load_c(2)
+        load_wgt()
         nc.sync.dma_start(offsets[:], offs)
-        nc.sync.dma_start(out=wgt_sb, in_=wgt)
         load_x(0)
         load_x(1)
-        load_scales(wx_sc, wx_scales)
+        load_scales(wt_sc, wt_scales)
         load_x(2)
         load_wx()
-        load_scales(wt_sc, wt_scales)
+        load_scales(wx_sc, wx_scales)
         load_x(3)
-        load_wt()
         load_c(3)
+        load_wt()
         load_bias()
 
         whole = places(0, 2)
@@ -198,7 +231,7 @@ def tile_list_gelu_kernel(
 
         def left_over(q, s):
             nc.vector.tensor_tensor(
-                out=by_runs_woven(woven("left", q)[:, places(s), :]),
+                out=by_runs_woven(woven_part("left", q, places(s))),
                 in0=by_runs_planes(c_tile(q)[:, :, places(s)]),
                 in1=by_runs_planes(backs[q, s][:]),
                 op=ALU.subtract,
@@ -210,18 +243,16 @@ def tile_list_gelu_kernel(
             nc.vector.tensor_tensor(
                 out=target[:, t, at : at + width],
                 in0=x_planes[t][:].indirect(offsets[:, start // 16 : (start + width) // 16]),
-                in1=wgt_sb[:, start : start + width],
+                in1=wgt_sb[start // HALF][:, start % HALF : start % HALF + width],
                 op=ALU.mult,
             )
 
-        def pick_plane(t):
-            pick(t, 0, 2)
-            pick(t, 2)
-            pick(t, 3)
-
-        def weave_x(copy, q):
+        def weave_x(copy, q, cols=whole):
             source, at = picked(q)
-            copy(out=by_runs_woven(woven("xw", q)), in_=by_runs_planes(source[:, :, at : at + CHUNK]))
+            copy(
+                out=by_runs_woven(woven("xw", q)[:, cols, :]),
+                in_=by_runs_planes(source[:, :, at + cols.start : at + cols.stop]),
+            )
 
         accs = {}
 
@@ -268,11 +299,15 @@ def tile_list_gelu_kernel(
         first_tier(1)
         left_over(0, 1)
         left_over(0, 0)
+        spread_wgt(0)
+        spread_wgt(1)
         left_over(1, 0)
         first_tier(2)
         left_over(1, 1)
+        turn_wgt(0)
         quantize("cr", "left", 0, whole)
         left_over(2, 0)
+        turn_wgt(1)
         left_over(2, 1)
         quantize("cr", "left", 1, whole)
         pick(0, 0, 2)
@@ -280,48 +315,48 @@ def tile_list_gelu_kernel(
         pick(0, 2)
         pick(0, 3)
         pick(1, 0, 2)
-        pick(1, 2)
         pick(2, 0, 2)
-        for q in range(3):
-            for s in range(2):
-                project("cq", q, s, start=True)
-                project("cr", q, s)
         pick(3, 0)
         weave_x(on_scalar, 0)
+        weave_c(on_scalar, 3, whole)
         pick(3, 1)
         weave_x(on_scalar, 1)
-        weave_c(on_scalar, 3, whole)
-        pick(2, 2)
-        pick(3, 2)
-        quantize("xq", "xw", 0, whole)
-        for s in range(2):
-            project("xq", 0, s, stop=True)
+        for t in range(1, PACK):
+            pick(t, 2)
         weave_x(on_scalar, 2)
-        finish(0, 0)
-        finish(0, 1)
+
+
+        def open_sums(q):
+            for s in range(2):
+                project("cq", q, s, start=True)
+                if q < CHUNKS - 1:
+                    project("cr", q, s)
+
+
+        def close_sums(q):
+            quantize("xq", "xw", q, whole)
+            for s in range(2):
+                project("xq", q, s, stop=True)
+                finish(q, s)
+
+
+        for q in range(CHUNKS - 1):
+            open_sums(q)
+        close_sums(0)
         pick(1, 3)
-        quantize("xq", "xw", 1, whole)
-        for s in range(2):
-            project("xq", 1, s, stop=True)
-            finish(1, s)
-        pick(2, 3)
         first_tier(3)
-        for s in range(2):
-            project("cq", 3, s, start=True)
+        close_sums(1)
+        pick(2, 3)
         pick(3, 3)
-        quantize("xq", "xw", 2, whole)
-        for s in range(2):
-            project("xq", 2, s, stop=True)
-            finish(2, s)
         left_over(3, 0)
-        weave_x(on_vector, 3)
-        quantize("cr", "left", 3, places(0))
-        project("cr", 3, 0)
-        quantize("xq", "xw", 3, whole)
-        project("xq", 3, 0, stop=True)
-        finish(3, 0)
-        left_over(3, 1)
-        project("xq", 3, 1)
-        quantize("cr", "left", 3, places(1))
-        project("cr", 3, 1, stop=True)
-        finish(3, 1)
+        close_sums(2)
+        open_sums(3)
+        for s in range(2):
+            if s == 1:
+                left_over(3, s)
+            weave_x(on_vector, 3, places(s))
+            quantize("cr", "left", 3, places(s))
+            project("cr", 3, s)
+            quantize("xq", "xw", 3, places(s))
+            project("xq", 3, s, stop=True)
+            finish(3, s)

@@ -37,7 +37,7 @@ def tile_list_gelu_kernel(
         laid = ctx.enter_context(tc.tile_pool(name="laid", bufs=1))
         psum = ctx.enter_context(tc.psum_pool(name="psum", bufs=1))
 
-        laid_at = {"eye": 0, "cw0_0": 0, "cw1": 1024, "cq0_scales": 3072, "cw2": 4032, "c0": 8192, "cq2_scales": 8192, "c2": 12544, "front": 16576}
+        laid_at = {"eye": 4032, "cw0_0": 4096, "cw1": 5120, "cq0_scales": 7168, "cw2": 8064, "c0": 10240, "cq2_scales": 10240, "spread1": 10496, "c2": 14336, "front": 18368}
 
         def tile(name, shape, dtype, tag=None):
             if name in laid_at:
@@ -67,19 +67,29 @@ def tile_list_gelu_kernel(
         wx_sc = tile("wx_sc", [P, N], U8)
         bias = tile("bias", [P, N // P], F32)
 
+        band = tile("band", [P, L + PACK], BF16)
+        nc.gpsimd.memset(band[:].bitcast(I32), 0)
+        nc.gpsimd.affine_select(
+            out=band[:],
+            in_=band[:],
+            compare_op=ALU.not_equal,
+            fill=1.0,
+            base=PACK - 1,
+            pattern=[[-1, L + PACK]],
+            channel_multiplier=PACK,
+        )
         ident = tile("ident", [P, P], F32)
         make_identity(nc, ident[:])
         warm = tile("warm", [P, 2], F32)
         nc.vector.memset(warm[:, 0:1], 0.0)
         nc.scalar.activation(out=warm[:, 1:2], in_=warm[:, 0:1], func=GELU)
 
-        eye = tile("eye", [P, PACK * (L + 2)], BF16)
+        eye = tile("eye", [P, PACK * L], BF16)
         eye_q = mx_tiles("eye", L)
-        nc.vector.memset(eye[:].bitcast(I32), 0)
         nc.vector.memset(wx_sc[:].bitcast(I32), 0)
         nc.vector.memset(wt_sc[:].bitcast(I32), 0)
-        slots = eye[:, 0 : PACK * (L + 1)].rearrange("p (t r) -> p t r", t=PACK)[:, :, 0:L:PACK]
-        nc.vector.tensor_copy(out=slots, in_=ident[:].unsqueeze(1).to_broadcast([P, PACK, P]))
+        for t in range(PACK):
+            nc.vector.tensor_copy(out=eye[:, t * L : (t + 1) * L], in_=band[:, PACK - 1 - t : PACK - 1 - t + L])
         nc.vector.quantize_mx(out=eye_q[0][:].bitcast(FP8X4), scales=eye_q[1][:], in_=eye[:, 0 : PACK * L])
 
         c_rows = c.rearrange("(p t) j -> p t j", t=PACK)
@@ -149,13 +159,13 @@ def tile_list_gelu_kernel(
 
         def load_wgt():
             rows = wgt.rearrange("(g r) (b j) -> (r b) g j", r=GROUP, j=P)
-            nc.sync.dma_start(out=wgt_rows[:], in_=rows[0:GROUP])
+            nc.scalar.dma_start(out=wgt_rows[:], in_=rows[0:GROUP])
 
         turned = {}
 
         def spread_wgt(h):
             if not turned:
-                turned["rows"] = bank(1, [P, GROUP, P // GROUP])
+                turned["rows"] = bank(6, [P, GROUP, P // GROUP])
                 nc.tensor.transpose(turned["rows"][:].rearrange("p b g -> p (b g)"), wgt_rows[:], ident[:])
             blocks = HALF // P
             spread = tile("spread%d" % h, [P, blocks, P // GROUP, GROUP], F32)
@@ -164,32 +174,34 @@ def tile_list_gelu_kernel(
             turned[h] = spread
 
         def turn_wgt(h):
-            back = bank(3 + h, [P, HALF])
+            back = bank(1 + 2 * h, [P, HALF])
             for block in range(HALF // P):
                 nc.tensor.transpose(
                     back[:, places(block)], turned[h][:, block, :, :].rearrange("p g r -> p (g r)"), ident[:]
                 )
             nc.scalar.copy(out=wgt_sb[h], in_=back[:])
 
-        def load_wx():
-            nc.sync.dma_start(out=wx_sb[:].bitcast(I32), in_=wx_words[0].rearrange("p n t -> p (n t)").bitcast(I32))
+        def load_wx(s):
+            words = wx_words[0].rearrange("p n t -> p (n t)").bitcast(I32)
+            nc.sync.dma_start(out=wx_sb[:, places(2 * s, 2)].bitcast(I32), in_=words[:, places(2 * s, 2)])
 
         def load_wt():
             nc.sync.dma_start(out=wt_sb[:].bitcast(I32), in_=wt_words[0].bitcast(I32))
 
+        load_wgt()
         load_c(0)
         load_c(1)
         load_c(2)
-        load_wgt()
         nc.sync.dma_start(offsets[:], offs)
         load_x(0)
         load_x(1)
         load_scales(wt_sc, wt_scales)
         load_x(2)
-        load_wx()
+        load_wx(0)
         load_scales(wx_sc, wx_scales)
         load_x(3)
         load_c(3)
+        load_wx(1)
         load_wt()
         load_bias()
 
@@ -293,21 +305,21 @@ def tile_list_gelu_kernel(
         weave_c(on_scalar, 0, places(1))
         first_tier(0, 0)
         first_tier(0, 1)
+        spread_wgt(0)
         weave_c(on_vector, 1, places(0))
         weave_c(on_scalar, 1, places(1))
         weave_c(on_scalar, 2, whole)
         first_tier(1)
         left_over(0, 1)
         left_over(0, 0)
-        spread_wgt(0)
+        turn_wgt(0)
         spread_wgt(1)
         left_over(1, 0)
         first_tier(2)
         left_over(1, 1)
-        turn_wgt(0)
+        turn_wgt(1)
         quantize("cr", "left", 0, whole)
         left_over(2, 0)
-        turn_wgt(1)
         left_over(2, 1)
         quantize("cr", "left", 1, whole)
         pick(0, 0, 2)
@@ -326,13 +338,6 @@ def tile_list_gelu_kernel(
         weave_x(on_scalar, 2)
 
 
-        def open_sums(q):
-            for s in range(2):
-                project("cq", q, s, start=True)
-                if q < CHUNKS - 1:
-                    project("cr", q, s)
-
-
         def close_sums(q):
             quantize("xq", "xw", q, whole)
             for s in range(2):
@@ -340,8 +345,10 @@ def tile_list_gelu_kernel(
                 finish(q, s)
 
 
-        for q in range(CHUNKS - 1):
-            open_sums(q)
+        for s in range(2):
+            for q in range(CHUNKS - 1):
+                project("cq", q, s, start=True)
+                project("cr", q, s)
         close_sums(0)
         pick(1, 3)
         first_tier(3)
@@ -350,7 +357,8 @@ def tile_list_gelu_kernel(
         pick(3, 3)
         left_over(3, 0)
         close_sums(2)
-        open_sums(3)
+        for s in range(2):
+            project("cq", 3, s, start=True)
         for s in range(2):
             if s == 1:
                 left_over(3, s)

@@ -291,14 +291,21 @@ def tile_list_gelu_kernel(
                 )
 
         def finish(q, s):
-            last = q == CHUNKS - 1
-            tiles = range(PACK) if last else range(2 * s, 2 * s + 2)
-            cols = places(2 * q + s) if last else places(2 * q, 2)
-            result = tile("result%d_%d" % (q, s), [P, PACK, STRIP] if last else [P, 2, CHUNK], F32)
-            for i, u in enumerate(tiles):
-                nc.scalar.activation(out=result[:, i, :], in_=accs[q, s][:, i, :], func=GELU, bias=bias[:, u : u + 1])
-                if i % 2 == 1:
-                    nc.sync.dma_start(out=out_rows[:, u - 1 : u + 1, cols], in_=result[:, i - 1 : i + 1, :])
+            if q < CHUNKS - 1:
+                result = tile("result%d_%d" % (q, s), [P, 2, CHUNK], F32)
+                for i, u in enumerate(range(2 * s, 2 * s + 2)):
+                    nc.scalar.activation(
+                        out=result[:, i, :], in_=accs[q, s][:, i, :], func=GELU, bias=bias[:, u : u + 1]
+                    )
+                nc.sync.dma_start(out=out_rows[:, 2 * s : 2 * s + 2, places(2 * q, 2)], in_=result[:])
+                return
+            result = once("result_last", [P, PACK, CHUNK], F32)
+            for u in range(PACK):
+                nc.scalar.activation(
+                    out=result[:, u, places(s)], in_=accs[q, s][:, u, :], func=GELU, bias=bias[:, u : u + 1]
+                )
+                if s == 1:
+                    nc.sync.dma_start(out=out_rows[:, u, places(2 * q, 2)], in_=result[:, u, :])
 
         on_vector, on_scalar = nc.vector.tensor_copy, nc.scalar.copy
         weave_c(on_vector, 0, places(0))

@@ -37,7 +37,7 @@ def tile_list_gelu_kernel(
         laid = ctx.enter_context(tc.tile_pool(name="laid", bufs=1))
         psum = ctx.enter_context(tc.psum_pool(name="psum", bufs=1))
 
-        laid_at = {"eye": 4032, "cw0_0": 4096, "cw1": 5120, "cq0_scales": 7168, "cw2": 8064, "c0": 10240, "cq2_scales": 10240, "spread1": 10496, "c2": 14336, "front": 18368}
+        laid_at = {"eye": 0, "cw0_0": 0, "cw1": 1024, "cq0_scales": 3072, "cw2": 4032, "c0": 8192, "cq2_scales": 8192, "c2": 12544, "front": 16576}
 
         def tile(name, shape, dtype, tag=None):
             if name in laid_at:
@@ -159,13 +159,13 @@ def tile_list_gelu_kernel(
 
         def load_wgt():
             rows = wgt.rearrange("(g r) (b j) -> (r b) g j", r=GROUP, j=P)
-            nc.scalar.dma_start(out=wgt_rows[:], in_=rows[0:GROUP])
+            nc.sync.dma_start(out=wgt_rows[:], in_=rows[0:GROUP])
 
         turned = {}
 
         def spread_wgt(h):
             if not turned:
-                turned["rows"] = bank(6, [P, GROUP, P // GROUP])
+                turned["rows"] = bank(1, [P, GROUP, P // GROUP])
                 nc.tensor.transpose(turned["rows"][:].rearrange("p b g -> p (b g)"), wgt_rows[:], ident[:])
             blocks = HALF // P
             spread = tile("spread%d" % h, [P, blocks, P // GROUP, GROUP], F32)
@@ -174,7 +174,7 @@ def tile_list_gelu_kernel(
             turned[h] = spread
 
         def turn_wgt(h):
-            back = bank(1 + 2 * h, [P, HALF])
+            back = bank(3 + h, [P, HALF])
             for block in range(HALF // P):
                 nc.tensor.transpose(
                     back[:, places(block)], turned[h][:, block, :, :].rearrange("p g r -> p (g r)"), ident[:]
@@ -188,10 +188,10 @@ def tile_list_gelu_kernel(
         def load_wt():
             nc.sync.dma_start(out=wt_sb[:].bitcast(I32), in_=wt_words[0].bitcast(I32))
 
-        load_wgt()
         load_c(0)
         load_c(1)
         load_c(2)
+        load_wgt()
         nc.sync.dma_start(offsets[:], offs)
         load_x(0)
         load_x(1)
@@ -312,21 +312,21 @@ def tile_list_gelu_kernel(
         weave_c(on_scalar, 0, places(1))
         first_tier(0, 0)
         first_tier(0, 1)
-        spread_wgt(0)
         weave_c(on_vector, 1, places(0))
         weave_c(on_scalar, 1, places(1))
         weave_c(on_scalar, 2, whole)
         first_tier(1)
         left_over(0, 1)
         left_over(0, 0)
-        turn_wgt(0)
+        spread_wgt(0)
         spread_wgt(1)
         left_over(1, 0)
         first_tier(2)
         left_over(1, 1)
-        turn_wgt(1)
+        turn_wgt(0)
         quantize("cr", "left", 0, whole)
         left_over(2, 0)
+        turn_wgt(1)
         left_over(2, 1)
         quantize("cr", "left", 1, whole)
         pick(0, 0, 2)

@@ -267,27 +267,33 @@ def tile_list_gelu_kernel(
             )
 
         accs = {}
+        last_banks = (1, 6, 2, 3)
 
         def project(name, q, s, start=False, stop=False):
             last = q == CHUNKS - 1
+            apart = last and s == 1
             tiles = range(PACK) if last else range(2 * s, 2 * s + 2)
             cols = places(s) if last else whole
-            if start:
-                accs[q, s] = bank(2 * (q % (CHUNKS - 1)) + s, [P, PACK, STRIP] if last else [P, 2, CHUNK])
             codes, scales = quantised[name][q]
             for i, u in enumerate(tiles):
+                if start and apart:
+                    accs[q, s, u] = bank(last_banks[u], [P, STRIP])[:]
+                elif start:
+                    if i == 0:
+                        shared = bank(2 * (q % (CHUNKS - 1)) + s, [P, PACK, STRIP] if last else [P, 2, CHUNK])
+                    accs[q, s, u] = shared[:, i, :]
                 if name == "xq":
                     words, plane = wt_sb[:, 2 * u * P : 2 * (u + 1) * P].bitcast(FP4X4), wt_sc
                 else:
                     words, plane = wx_sb[:, places(u)].bitcast(FP8X4), wx_sc
                 nc.tensor.matmul_mx(
-                    out=accs[q, s][:, i, :],
+                    out=accs[q, s, u],
                     lhsT=words,
                     lhsT_scale=plane[:, places(u)],
                     rhs=codes[:, cols].bitcast(FP8X4),
                     rhs_scale=scales[:, cols],
-                    start=(start and i == 0),
-                    stop=(stop and i == len(tiles) - 1),
+                    start=(start and (apart or i == 0)),
+                    stop=(stop and (apart or i == len(tiles) - 1)),
                 )
 
         def finish(q, s):
@@ -295,14 +301,14 @@ def tile_list_gelu_kernel(
                 result = tile("result%d_%d" % (q, s), [P, 2, CHUNK], F32)
                 for i, u in enumerate(range(2 * s, 2 * s + 2)):
                     nc.scalar.activation(
-                        out=result[:, i, :], in_=accs[q, s][:, i, :], func=GELU, bias=bias[:, u : u + 1]
+                        out=result[:, i, :], in_=accs[q, s, u], func=GELU, bias=bias[:, u : u + 1]
                     )
                 nc.sync.dma_start(out=out_rows[:, 2 * s : 2 * s + 2, places(2 * q, 2)], in_=result[:])
                 return
             result = once("result_last", [P, PACK, CHUNK], F32)
             for u in range(PACK):
                 nc.scalar.activation(
-                    out=result[:, u, places(s)], in_=accs[q, s][:, u, :], func=GELU, bias=bias[:, u : u + 1]
+                    out=result[:, u, places(s)], in_=accs[q, s, u], func=GELU, bias=bias[:, u : u + 1]
                 )
                 if s == 1:
                     nc.sync.dma_start(out=out_rows[:, u, places(2 * q, 2)], in_=result[:, u, :])

@@ -343,12 +343,13 @@ def tile_list_gelu_kernel(
         pick(2, 0, 2)
         pick(3, 0)
         weave_x(on_scalar, 0)
-        weave_c(on_scalar, 3, whole)
+        weave_c(on_scalar, 3, places(1))
         pick(3, 1)
         weave_x(on_scalar, 1)
         for t in range(1, PACK):
             pick(t, 2)
         weave_x(on_scalar, 2)
+        weave_c(on_vector, 3, places(0))
 
 
         def close_sums(q):

@@ -144,7 +144,7 @@ def tile_list_gelu_kernel(
             if (name, q) == ("cw", 0):
                 return once("cw0_%d" % (cols.start // STRIP), [P, STRIP, PACK], BF16)[:]
             if (name, q) == ("left", CHUNKS - 1):
-                return as_woven(front()[:, PACK * HALF :] if cols.start == 0 else third()[:, CHUNK : 2 * CHUNK])
+                return as_woven(third()[:, CHUNK : 3 * CHUNK])[:, cols, :]
             return woven(name, q)[:, cols, :]
 
         def load_c(q):
@@ -343,13 +343,13 @@ def tile_list_gelu_kernel(
         pick(2, 0, 2)
         pick(3, 0)
         weave_x(on_scalar, 0)
-        weave_c(on_scalar, 3, places(1))
+        weave_c(on_scalar, 3, slice(CHUNK // 4, CHUNK))
         pick(3, 1)
         weave_x(on_scalar, 1)
         for t in range(1, PACK):
             pick(t, 2)
         weave_x(on_scalar, 2)
-        weave_c(on_vector, 3, places(0))
+        weave_c(on_vector, 3, slice(0, CHUNK // 4))
 
 
         def close_sums(q):
@@ -369,8 +369,8 @@ def tile_list_gelu_kernel(
         close_sums(1)
         pick(2, 3)
         pick(3, 3)
-        left_over(3, 0)
         close_sums(2)
+        left_over(3, 0)
         for s in range(2):
             project("cq", 3, s, start=True)
         for s in range(2):

@@ -86,6 +86,8 @@ def tile_list_gelu_kernel(
 
         eye = tile("eye", [P, PACK * L], BF16)
         eye_q = mx_tiles("eye", L)
+        wgt_rows = tile("wgt_rows", [P, P], F32)
+        nc.vector.memset(wgt_rows[P // 2 :, :], 0.0)
         nc.vector.memset(wx_sc[:].bitcast(I32), 0)
         nc.vector.memset(wt_sc[:].bitcast(I32), 0)
         for t in range(PACK):
@@ -155,22 +157,24 @@ def tile_list_gelu_kernel(
 
         wgt_sb = [third()[:, 2 * CHUNK : 4 * CHUNK], tile("wgt1", [P, HALF], F32)[:]]
 
-        wgt_rows = tile("wgt_rows", [P, P], F32)
-
         def load_wgt():
-            rows = wgt.rearrange("(g r) (b j) -> (r b) g j", r=GROUP, j=P)
-            nc.sync.dma_start(out=wgt_rows[:], in_=rows[0:GROUP])
+            rows = wgt.rearrange("(g r) (b j) -> (r b) g j", r=2 * GROUP, j=P)
+            nc.sync.dma_start(out=wgt_rows[0 : P // 2, :], in_=rows[:: GROUP + 1])
 
         turned = {}
 
         def spread_wgt(h):
             if not turned:
-                turned["rows"] = bank(1, [P, GROUP, P // GROUP])
-                nc.tensor.transpose(turned["rows"][:].rearrange("p b g -> p (b g)"), wgt_rows[:], ident[:])
-            blocks = HALF // P
-            spread = tile("spread%d" % h, [P, blocks, P // GROUP, GROUP], F32)
-            columns = turned["rows"][:, h * blocks : (h + 1) * blocks, :]
-            nc.scalar.copy(out=spread[:], in_=columns.unsqueeze(3).to_broadcast([P, blocks, P // GROUP, GROUP]))
+                turned["rows"] = bank(1, [P, P])
+                nc.tensor.transpose(turned["rows"][:], wgt_rows[:], ident[:])
+            blocks, groups = HALF // P, P // GROUP
+            spread = tile("spread%d" % h, [P, blocks, groups, GROUP], F32)
+            columns = turned["rows"][:, 0 : P // 2].rearrange("p (o b g) -> p b g o", o=2, g=groups // 2)
+            shape = [P, blocks, groups // 2, 2, GROUP]
+            nc.scalar.copy(
+                out=spread[:].rearrange("p b (g o) r -> p b g o r", o=2),
+                in_=columns[:, h * blocks : (h + 1) * blocks, :, :].unsqueeze(4).to_broadcast(shape),
+            )
             turned[h] = spread
 
         def turn_wgt(h):

from contextlib import ExitStack

import concourse.mybir as mybir
from concourse.masks import make_identity

K, L, N, T, J = 512, 512, 512, 2048, 1024
FLOPS = 2 * N * J * (K + 2 * L) + 2 * L * L * J

F32 = mybir.dt.float32
BF16 = mybir.dt.bfloat16
I32 = mybir.dt.int32
U32 = mybir.dt.uint32
U16 = mybir.dt.uint16
U8 = mybir.dt.uint8
FP8X4 = mybir.dt.float8_e4m3fn_x4
FP4X4 = mybir.dt.float4_e2m1fn_x4
ALU = mybir.AluOpType
GELU = mybir.ActivationFunctionType.Gelu_apprx_tanh

P = 128
PACK = 4
QUAD = 32
STRIP = 128
CHUNK = 2 * STRIP
CHUNKS = J // CHUNK
HALF = J // 2
RUN = 2
GROUP = 16


def tile_list_gelu_kernel(
    tc, xT, wgt, wt_words, wt_scales, c, wx_words, wx_scales, b, offs, out
):
    nc = tc.nc
    with ExitStack() as ctx:
        keep = ctx.enter_context(tc.tile_pool(name="keep", bufs=1))
        laid = ctx.enter_context(tc.tile_pool(name="laid", bufs=1))
        psum = ctx.enter_context(tc.psum_pool(name="psum", bufs=1))

        laid_at = {"eye": 0, "cw0_0": 0, "cw1": 1024, "cq0_scales": 3072, "cw2": 4032, "c0": 8192, "cq2_scales": 8192, "c2": 12544, "front": 16576}

        def tile(name, shape, dtype, tag=None):
            if name in laid_at:
                return laid.tile(shape, dtype, name=name, align_bytes=64, offset=laid_at[name])
            return keep.tile(shape, dtype, name=name, tag=tag or name, align_bytes=64)

        def bank(index, shape):
            return psum.tile(shape, F32, name="bank%d" % index, tag="bank%d" % index)

        def mx_tiles(name, width):
            return tile(name + "_codes", [P, width], U32), tile(name + "_scales", [P, width], U8)

        def by_runs_planes(planes):
            return planes.rearrange("p t (c i) -> p c t i", i=RUN)

        def by_runs_woven(woven):
            return woven.rearrange("p (c i) t -> p c t i", i=RUN)

        def places(first, count=1):
            return slice(first * STRIP, (first + count) * STRIP)

        offsets = keep.tile([P, J // 16], U16, name="offsets")
        x_planes = [tile("x%d" % t, [P, T], F32) for t in range(PACK)]
        wt_sb = tile("wt_sb", [P, 2 * N], U8)
        wx_sb = tile("wx_sb", [P, N], U32)
        wt_sc = tile("wt_sc", [P, N], U8)
        wx_sc = tile("wx_sc", [P, N], U8)
        bias = tile("bias", [P, N // P], F32)

        band = tile("band", [P, L + PACK], BF16)
        nc.gpsimd.memset(band[:].bitcast(I32), 0)
        nc.gpsimd.affine_select(
            out=band[:],
            in_=band[:],
            compare_op=ALU.not_equal,
            fill=1.0,
            base=PACK - 1,
            pattern=[[-1, L + PACK]],
            channel_multiplier=PACK,
        )
        ident = tile("ident", [P, P], F32)
        make_identity(nc, ident[:])
        warm = tile("warm", [P, 2], F32)
        nc.vector.memset(warm[:, 0:1], 0.0)
        nc.scalar.activation(out=warm[:, 1:2], in_=warm[:, 0:1], func=GELU)

        eye = tile("eye", [P, PACK * L], BF16)
        eye_q = mx_tiles("eye", L)
        wgt_rows = tile("wgt_rows", [P, P], F32)
        nc.vector.memset(wgt_rows[P // 2 :, :], 0.0)
        nc.vector.memset(wx_sc[:].bitcast(I32), 0)
        nc.vector.memset(wt_sc[:].bitcast(I32), 0)
        for t in range(PACK):
            nc.vector.tensor_copy(out=eye[:, t * L : (t + 1) * L], in_=band[:, PACK - 1 - t : PACK - 1 - t + L])
        nc.vector.quantize_mx(out=eye_q[0][:].bitcast(FP8X4), scales=eye_q[1][:], in_=eye[:, 0 : PACK * L])

        c_rows = c.rearrange("(p t) j -> p t j", t=PACK)
        x_rows = xT.rearrange("(p t) s -> p t s", t=PACK)
        out_rows = out.rearrange("(u p) j -> p u j", p=P)

        def load_scales(plane, rows):
            for quad in range(P // QUAD):
                nc.sync.dma_start(
                    out=plane[QUAD * quad : QUAD * quad + 4, :].bitcast(I32),
                    in_=rows[0, 4 * quad : 4 * quad + 4, :].bitcast(I32),
                )

        def load_bias():
            with nc.allow_non_contiguous_dma(reason="one bias value for each partition"):
                nc.sync.dma_start(out=bias[:], in_=b.rearrange("(u p) -> p u", p=P))

        tags = {}
        made = {}

        def once(name, shape, dtype):
            if name not in made:
                made[name] = tile(name, shape, dtype, tags.get(name))
            return made[name]

        def c_tile(q):
            return once("c%d" % q, [P, PACK, CHUNK], F32)

        def front():
            return once("front", [P, CHUNK + PACK * HALF], F32)

        def third():
            return once("third", [P, (PACK + 1) * CHUNK], F32)

        def as_planes(words):
            return words.rearrange("p (t j) -> p t j", t=PACK)

        def as_woven(words):
            return words.bitcast(BF16).rearrange("p (j t) -> p j t", t=PACK)

        def picked(q):
            if q < 2:
                return as_planes(front()[:, CHUNK:]), q * CHUNK
            return as_planes(third()[:, CHUNK:] if q == 2 else front()[:, 0 : PACK * CHUNK]), 0

        def woven(name, q):
            if (name, q) == ("left", 1):
                return as_woven(third()[:, 0 : 2 * CHUNK])
            return once("%s%d" % (name, q), [P, CHUNK, PACK], BF16)[:]

        def woven_part(name, q, cols):
            if (name, q) == ("cw", 0):
                return once("cw0_%d" % (cols.start // STRIP), [P, STRIP, PACK], BF16)[:]
            if (name, q) == ("left", CHUNKS - 1):
                return as_woven(third()[:, CHUNK : 3 * CHUNK])[:, cols, :]
            return woven(name, q)[:, cols, :]

        def load_c(q):
            nc.sync.dma_start(out=c_tile(q)[:], in_=c_rows[:, :, places(2 * q, 2)])

        def load_x(t):
            nc.sync.dma_start(out=x_planes[t][:], in_=x_rows[:, t, :])

        wgt_sb = [third()[:, 2 * CHUNK : 4 * CHUNK], tile("wgt1", [P, HALF], F32)[:]]

        def load_wgt():
            rows = wgt.rearrange("(g r) (b j) -> (r b) g j", r=2 * GROUP, j=P)
            nc.sync.dma_start(out=wgt_rows[0 : P // 2, :], in_=rows[:: GROUP + 1])

        turned = {}

        def spread_wgt(h):
            if not turned:
                turned["rows"] = bank(1, [P, P])
                nc.tensor.transpose(turned["rows"][:], wgt_rows[:], ident[:])
            blocks, groups = HALF // P, P // GROUP
            spread = tile("spread%d" % h, [P, blocks, groups, GROUP], F32)
            columns = turned["rows"][:, 0 : P // 2].rearrange("p (o b g) -> p b g o", o=2, g=groups // 2)
            shape = [P, blocks, groups // 2, 2, GROUP]
            nc.scalar.copy(
                out=spread[:].rearrange("p b (g o) r -> p b g o r", o=2),
                in_=columns[:, h * blocks : (h + 1) * blocks, :, :].unsqueeze(4).to_broadcast(shape),
            )
            turned[h] = spread

        def turn_wgt(h):
            back = bank(3 + h, [P, HALF])
            for block in range(HALF // P):
                nc.tensor.transpose(
                    back[:, places(block)], turned[h][:, block, :, :].rearrange("p g r -> p (g r)"), ident[:]
                )
            nc.scalar.copy(out=wgt_sb[h], in_=back[:])

        def load_wx(s):
            words = wx_words[0].rearrange("p n t -> p (n t)").bitcast(I32)
            nc.sync.dma_start(out=wx_sb[:, places(2 * s, 2)].bitcast(I32), in_=words[:, places(2 * s, 2)])

        def load_wt():
            nc.sync.dma_start(out=wt_sb[:].bitcast(I32), in_=wt_words[0].bitcast(I32))

        load_c(0)
        load_c(1)
        load_c(2)
        load_wgt()
        nc.sync.dma_start(offsets[:], offs)
        load_x(0)
        load_x(1)
        load_scales(wt_sc, wt_scales)
        load_x(2)
        load_wx(0)
        load_scales(wx_sc, wx_scales)
        load_x(3)
        load_c(3)
        load_wx(1)
        load_wt()
        load_bias()

        whole = places(0, 2)
        quantised = {name: [mx_tiles("%s%d" % (name, q), CHUNK) for q in range(CHUNKS)] for name in ("cq", "cr", "xq")}

        def quantize(name, source, q, cols):
            codes, scales = quantised[name][q]
            nc.vector.quantize_mx(
                out=codes[:, cols].bitcast(FP8X4),
                scales=scales[:, cols],
                in_=woven_part(source, q, cols).rearrange("p j t -> p (j t)"),
            )


        def weave_c(copy, q, cols):
            copy(out=by_runs_woven(woven_part("cw", q, cols)), in_=by_runs_planes(c_tile(q)[:, :, cols]))

        backs = {}

        def bring_back(q, s):
            backs[q, s] = bank(2 * q + s, [P, PACK, STRIP])
            codes, scales = quantised["cq"][q]
            for t in range(PACK):
                nc.tensor.matmul_mx(
                    out=backs[q, s][:, t, :],
                    lhsT=eye_q[0][:, places(t)].bitcast(FP8X4),
                    lhsT_scale=eye_q[1][:, places(t)],
                    rhs=codes[:, places(s)].bitcast(FP8X4),
                    rhs_scale=scales[:, places(s)],
                    start=True,
                    stop=True,
                )

        def first_tier(q, s=None):
            quantize("cq", "cw", q, whole if s is None else places(s))
            for strip in range(2) if s is None else (s,):
                bring_back(q, strip)

        def left_over(q, s):
            nc.vector.tensor_tensor(
                out=by_runs_woven(woven_part("left", q, places(s))),
                in0=by_runs_planes(c_tile(q)[:, :, places(s)]),
                in1=by_runs_planes(backs[q, s][:]),
                op=ALU.subtract,
            )

        def pick(t, q, count=1):
            target, at = picked(q)
            start, width = q * CHUNK, count * CHUNK
            nc.vector.tensor_tensor(
                out=target[:, t, at : at + width],
                in0=x_planes[t][:].indirect(offsets[:, start // 16 : (start + width) // 16]),
                in1=wgt_sb[start // HALF][:, start % HALF : start % HALF + width],
                op=ALU.mult,
            )

        def weave_x(copy, q, cols=whole):
            source, at = picked(q)
            copy(
                out=by_runs_woven(woven("xw", q)[:, cols, :]),
                in_=by_runs_planes(source[:, :, at + cols.start : at + cols.stop]),
            )

        accs = {}
        last_banks = (1, 6, 2, 3)

        def project(name, q, s, start=False, stop=False):
            last = q == CHUNKS - 1
            apart = last and s == 1
            tiles = range(PACK) if last else range(2 * s, 2 * s + 2)
            cols = places(s) if last else whole
            codes, scales = quantised[name][q]
            for i, u in enumerate(tiles):
                if start and apart:
                    accs[q, s, u] = bank(last_banks[u], [P, STRIP])[:]
                elif start:
                    if i == 0:
                        shared = bank(2 * (q % (CHUNKS - 1)) + s, [P, PACK, STRIP] if last else [P, 2, CHUNK])
                    accs[q, s, u] = shared[:, i, :]
                if name == "xq":
                    words, plane = wt_sb[:, 2 * u * P : 2 * (u + 1) * P].bitcast(FP4X4), wt_sc
                else:
                    words, plane = wx_sb[:, places(u)].bitcast(FP8X4), wx_sc
                nc.tensor.matmul_mx(
                    out=accs[q, s, u],
                    lhsT=words,
                    lhsT_scale=plane[:, places(u)],
                    rhs=codes[:, cols].bitcast(FP8X4),
                    rhs_scale=scales[:, cols],
                    start=(start and (apart or i == 0)),
                    stop=(stop and (apart or i == len(tiles) - 1)),
                )

        def finish(q, s):
            if q < CHUNKS - 1:
                result = tile("result%d_%d" % (q, s), [P, 2, CHUNK], F32)
                for i, u in enumerate(range(2 * s, 2 * s + 2)):
                    nc.scalar.activation(
                        out=result[:, i, :], in_=accs[q, s, u], func=GELU, bias=bias[:, u : u + 1]
                    )
                nc.sync.dma_start(out=out_rows[:, 2 * s : 2 * s + 2, places(2 * q, 2)], in_=result[:])
                return
            result = once("result_last", [P, PACK, CHUNK], F32)
            for u in range(PACK):
                nc.scalar.activation(
                    out=result[:, u, places(s)], in_=accs[q, s, u], func=GELU, bias=bias[:, u : u + 1]
                )
                if s == 1:
                    nc.sync.dma_start(out=out_rows[:, u, places(2 * q, 2)], in_=result[:, u, :])

        on_vector, on_scalar = nc.vector.tensor_copy, nc.scalar.copy
        weave_c(on_vector, 0, places(0))
        weave_c(on_scalar, 0, places(1))
        first_tier(0, 0)
        first_tier(0, 1)
        weave_c(on_vector, 1, places(0))
        weave_c(on_scalar, 1, places(1))
        weave_c(on_scalar, 2, whole)
        first_tier(1)
        left_over(0, 1)
        left_over(0, 0)
        spread_wgt(0)
        spread_wgt(1)
        left_over(1, 0)
        first_tier(2)
        left_over(1, 1)
        turn_wgt(0)
        quantize("cr", "left", 0, whole)
        left_over(2, 0)
        turn_wgt(1)
        left_over(2, 1)
        quantize("cr", "left", 1, whole)
        pick(0, 0, 2)
        quantize("cr", "left", 2, whole)
        pick(0, 2)
        pick(0, 3)
        pick(1, 0, 2)
        pick(2, 0, 2)
        pick(3, 0)
        weave_x(on_scalar, 0)
        weave_c(on_scalar, 3, slice(CHUNK // 4, CHUNK))
        pick(3, 1)
        weave_x(on_scalar, 1)
        for t in range(1, PACK):
            pick(t, 2)
        weave_x(on_scalar, 2)
        weave_c(on_vector, 3, slice(0, CHUNK // 4))


        def close_sums(q):
            quantize("xq", "xw", q, whole)
            for s in range(2):
                project("xq", q, s, stop=True)
                finish(q, s)


        for s in range(2):
            for q in range(CHUNKS - 1):
                project("cq", q, s, start=True)
                project("cr", q, s)
        close_sums(0)
        pick(1, 3)
        first_tier(3)
        close_sums(1)
        pick(2, 3)
        pick(3, 3)
        close_sums(2)
        left_over(3, 0)
        for s in range(2):
            project("cq", 3, s, start=True)
        for s in range(2):
            if s == 1:
                left_over(3, s)
            weave_x(on_vector, 3, places(s))
            quantize("cr", "left", 3, places(s))
            project("cr", 3, s)
            quantize("xq", "xw", 3, places(s))
            project("xq", 3, s, stop=True)
            finish(3, s)
